import numpy as np
import ml_dtypes


def mxq(x, axis, fmt="e4m3"):
    dtype, down = {"e4m3": (ml_dtypes.float8_e4m3fn, 7), "e5m2": (ml_dtypes.float8_e5m2, 14)}[fmt]
    v = np.moveaxis(np.asarray(x, np.float32).astype(ml_dtypes.bfloat16).astype(np.float64), axis, -1)
    blocks = v.reshape(v.shape[:-1] + (-1, 32))
    amax = np.abs(blocks).max(-1, keepdims=True)
    byte = np.maximum(np.where(amax > 0, np.frexp(amax)[1] - 1 + 127, 0) - down, 1)
    scale = np.exp2(byte - 127.0)
    codes = (blocks / scale).astype(np.float32).astype(dtype).astype(np.float64)
    return np.moveaxis((codes * scale).reshape(v.shape), -1, axis)


WIDE = False


def mx_kscale(k):
    if not WIDE:
        return np.ones(k)
    levels = np.array([10, -10, 5, -5, 0])
    if k % 512:
        return np.exp2(np.random.permutation(np.resize(levels, k // 32))).repeat(32)
    a = np.empty((k // 512, 16))
    for p in range(k // 512):
        a[p, :8] = np.random.permutation(np.resize(levels, 8))
        for g in range(8):
            far = levels[np.abs(levels - a[p, g]) >= 10]
            a[p, g + 8] = far[np.random.randint(len(far))]
    return np.exp2(a.ravel()).repeat(32)


def f64(x):
    return np.asarray(x).astype(np.float64)


def striped(idx):
    return np.tile(idx.reshape(-1, 16).T, (8, 1)).astype(np.uint16)


def unstriped(offs):
    return offs[:16].T.reshape(-1).astype(np.int64)


E2M1 = np.array([0.0, 0.5, 1.0, 1.5, 2.0, 3.0, 4.0, 6.0, -0.0, -0.5, -1.0, -1.5, -2.0, -3.0, -4.0, -6.0])


def pack_weight(w, fmt):
    k, n = w.shape
    w = f64(np.asarray(w, np.float32).astype(ml_dtypes.bfloat16)).reshape(k // 32, 32, n)
    amax = np.abs(w).max(1)
    if fmt == "e4m3":
        byte = np.frexp(amax)[1] - 1 + 127 - 7
    else:
        mant, ex = np.frexp(amax / 6.0)
        byte = np.where(mant > 0.5, ex, ex - 1) + 127
    byte = np.clip(np.where(amax > 0, byte, 1), 1, 254)
    scaled = (w * np.exp2(127.0 - byte)[:, None, :]).reshape(k, n).astype(np.float32)
    by_word = np.ascontiguousarray(scaled.reshape(k // 512, 128, 4, n).transpose(0, 1, 3, 2))
    if fmt == "e4m3":
        words = by_word.astype(ml_dtypes.float8_e4m3fn).view(np.uint8)
    else:
        c = by_word.astype(ml_dtypes.float4_e2m1fn).view(np.uint8) & 0xF
        words = (c[..., 0::2] | (c[..., 1::2] << 4)).reshape(k // 512, 128, 2 * n)
    return np.ascontiguousarray(words), np.ascontiguousarray(byte.astype(np.uint8).reshape(k // 512, 16, n))


def unpack_weight(words, scales, fmt):
    g, _, n = scales.shape
    words = np.ascontiguousarray(words).reshape(g, 128, n, -1)
    if fmt == "e4m3":
        vals = words.view(ml_dtypes.float8_e4m3fn).astype(np.float64)
    else:
        nib = np.empty((g, 128, n, 4), np.uint8)
        nib[..., 0::2] = words & 0xF
        nib[..., 1::2] = words >> 4
        vals = E2M1[nib]
    vals = vals * np.repeat(np.exp2(scales.astype(np.float64) - 127.0), 8, axis=1)[..., None]
    return vals.transpose(0, 1, 3, 2).reshape(g * 512, n)


def gelu(v):
    return 0.5 * v * (1.0 + np.tanh(np.sqrt(2.0 / np.pi) * (v + 0.044715 * v**3)))


K, T, S, P, H = 1536, 4096, 1024, 512, 1024


def setup_inputs():
    n = np.random.standard_normal
    s = mx_kscale(K)[:, None]
    u = mx_kscale(H)[:, None]
    tab_words, tab_scales = pack_weight(n((K, T)) * s, "e4m3")
    w1 = (n((K, H)) / np.sqrt(K) / s).astype(np.float32)
    w4_words, w4_scales = pack_weight(n((H, H)) / np.sqrt(H) / u, "e2m1")
    gain = (0.6 * np.exp(0.3 * n(H)) * u[:, 0]).astype(np.float32)
    return {
        "tab_words": tab_words, "tab_scales": tab_scales,
        "offs": striped(np.random.permutation(T)[:S]),
        "pos1": striped(np.random.permutation(S)[:P]),
        "pos2": striped(np.random.permutation(S)[:P]),
        "w1": w1, "w4_words": w4_words, "w4_scales": w4_scales,
        "gain": gain,
    }


def reference(tab_words, tab_scales, offs, pos1, pos2, w1, w4_words, w4_scales, gain):
    v = unpack_weight(tab_words, tab_scales, "e4m3")[:, unstriped(offs)]
    h = np.square(mxq(f64(w1), 0, "e4m3").T @ v)
    x = h[:, unstriped(pos1)] * f64(gain)[:, None]
    w4 = unpack_weight(w4_words, w4_scales, "e2m1")
    y = w4.T @ mxq(x, 0, "e4m3")
    return np.sqrt(np.square(y) + h[:, unstriped(pos2)] + 0.25)

@@ -1,0 +1,238 @@
+from contextlib import ExitStack
+
+import concourse.mybir as mybir
+
+K, T, S, PAIRS, H = 1536, 4096, 1024, 512, 1024
+FLOPS = 2 * K * H * S + 2 * H * H * PAIRS
+
+F32 = mybir.dt.float32
+BF16 = mybir.dt.bfloat16
+I32 = mybir.dt.int32
+U32 = mybir.dt.uint32
+U16 = mybir.dt.uint16
+U8 = mybir.dt.uint8
+FP8X4 = mybir.dt.float8_e4m3fn_x4
+FP4X4 = mybir.dt.float4_e2m1fn_x4
+ACT = mybir.ActivationFunctionType
+ALU = mybir.AluOpType
+
+P = 128
+PACK = 4
+SPAN = P * PACK
+K_PASSES = K // SPAN
+BLOCKS = H // SPAN
+HALVES = S // SPAN
+LIST_COLS = SPAN // 16
+
+
+def tile_list_titanium_shock_pairs_kernel(
+    tc, tab_words, tab_scales, offs, pos1, pos2, w1, w4_words, w4_scales, gain, out
+):
+    nc = tc.nc
+    with ExitStack() as ctx:
+        keep = ctx.enter_context(tc.tile_pool(name="keep", bufs=1))
+        stage = ctx.enter_context(tc.tile_pool(name="stage", bufs=3))
+        psum = ctx.enter_context(tc.psum_pool(name="psum", bufs=8))
+
+        offs_sb = keep.tile([P, S // 16], U16, name="offs_sb")
+        pos1_sb = keep.tile([P, PAIRS // 16], U16, name="pos1_sb")
+        pos2_sb = keep.tile([P, PAIRS // 16], U16, name="pos2_sb")
+        tab_w = [keep.tile([P, T], I32, name="tab_w%d" % a) for a in range(K_PASSES)]
+        tab_s = keep.tile([P, T], U8, name="tab_s")
+        w4_raw = keep.tile([P, BLOCKS, 2 * H], U8, name="w4_raw")
+        w4_raw_s = keep.tile([P, BLOCKS, H], U8, name="w4_raw_s")
+        w4_c = keep.tile([P, BLOCKS, 2 * H], U8, name="w4_c", align_bytes=64)
+        w4_s = keep.tile([P, BLOCKS, H], U8, name="w4_s", align_bytes=64)
+        gain_sb = keep.tile([P, BLOCKS, PACK], F32, name="gain_sb")
+        gain_rows = keep.tile([P, BLOCKS * PACK, PAIRS], F32, name="gain_rows")
+        eps = keep.tile([P, 1], F32, name="eps")
+        v_c = {}
+        v_s = keep.tile([P, S], U8, name="v_s", align_bytes=64)
+        w_raw, w_bf, w_c, w_s = {}, {}, {}, {}
+        h, acc, x_f, x_bf, x_c, x_s = {}, {}, {}, {}, {}, {}
+
+        def load_w1(a, b):
+            w_raw[a, b] = stage.tile([P, PACK, SPAN], F32, name="w_raw")
+            rows = w1[a * SPAN : (a + 1) * SPAN, b * SPAN : (b + 1) * SPAN]
+            nc.sync.dma_start(out=w_raw[a, b][:], in_=rows.rearrange("(p j) c -> p j c", j=PACK))
+
+        def load_tab(a):
+            nc.sync.dma_start(out=tab_w[a][:], in_=tab_words[a].rearrange("p t i -> p (t i)").bitcast(I32))
+
+        def cast_w1(a, b, m_vector):
+            w_bf[a, b] = stage.tile([P, PACK, P, PACK], BF16, name="w_bf", align_bytes=64)
+            dst = w_bf[a, b][:].rearrange("p t m j -> p m j t")
+            src = w_raw[a, b][:].rearrange("p j (m t) -> p m j t", t=PACK)
+            if m_vector > 0:
+                nc.vector.tensor_copy(out=dst[:, :m_vector], in_=src[:, :m_vector])
+            if m_vector < P:
+                nc.scalar.copy(out=dst[:, m_vector:], in_=src[:, m_vector:])
+
+        def quantize_w1(a, b):
+            w_c[a, b] = keep.tile([P, SPAN], U32, name="w_c%d%d" % (a, b), align_bytes=64)
+            w_s[a, b] = keep.tile([P, SPAN], U8, name="w_s%d%d" % (a, b), align_bytes=64)
+            nc.vector.quantize_mx(
+                out=w_c[a, b][:].bitcast(FP8X4),
+                scales=w_s[a, b][:],
+                in_=w_bf[a, b][:].rearrange("p t m j -> p (t m j)"),
+            )
+
+        def gather_tab(a, u):
+            v_c[a, u] = keep.tile([P, SPAN], U32, name="v_c%d%d" % (a, u), align_bytes=64)
+            picks = offs_sb[:, u * LIST_COLS : (u + 1) * LIST_COLS]
+            nc.vector.tensor_copy(v_c[a, u][:], tab_w[a][:].bitcast(U32).indirect(picks))
+
+        def first_pass(a, b, t, u):
+            if a == 0:
+                acc[b, t, u] = psum.tile([P, SPAN], F32, name="bank")
+            cols = slice(t * P, (t + 1) * P)
+            nc.tensor.matmul_mx(
+                out=acc[b, t, u][:],
+                lhsT=w_c[a, b][:, cols].bitcast(FP8X4),
+                lhsT_scale=w_s[a, b][:, cols],
+                rhs=v_c[a, u][:].bitcast(FP8X4),
+                rhs_scale=v_s[PACK * (a + 1) :, u * SPAN : (u + 1) * SPAN],
+                start=(a == 0),
+                stop=(a == K_PASSES - 1),
+            )
+
+        def square_h(b, t, u):
+            if u == 0:
+                h[b, t] = keep.tile([P, S], F32, name="h%d%d" % (b, t))
+            nc.scalar.activation(out=h[b, t][:, u * SPAN : (u + 1) * SPAN], in_=acc[b, t, u][:], func=ACT.Square)
+
+        def pick_x(b, t):
+            if t == 0:
+                x_f[b] = keep.tile([P, PACK, PAIRS], F32, name="x_f%d" % b)
+            nc.vector.tensor_tensor(
+                x_f[b][:, t, :], h[b, t][:].indirect(pos1_sb[:]), gain_rows[:, b * PACK + t, :], ALU.mult
+            )
+
+        def round_x(b, engine):
+            x_bf[b] = keep.tile([P, PAIRS * PACK], BF16, name="x_bf%d" % b, align_bytes=64)
+            dst = x_bf[b][:].rearrange("p (c i t) -> p c t i", i=4, t=PACK)
+            src = x_f[b][:].rearrange("p t (c i) -> p c t i", i=4)
+            if engine == "vector":
+                nc.vector.tensor_copy(out=dst, in_=src)
+            else:
+                nc.scalar.copy(out=dst, in_=src)
+
+        def quantize_x(b):
+            x_c[b] = keep.tile([P, PAIRS], U32, name="x_c%d" % b, align_bytes=64)
+            x_s[b] = keep.tile([P, PAIRS], U8, name="x_s%d" % b, align_bytes=64)
+            nc.vector.quantize_mx(out=x_c[b][:].bitcast(FP8X4), scales=x_s[b][:], in_=x_bf[b][:])
+
+        nc.vector.memset(tab_s[:].bitcast(I32), 0)
+        nc.vector.memset(w4_raw_s[:].bitcast(I32), 0)
+        nc.vector.memset(eps[:], 0.25)
+        def load_tab_scales(q):
+            nc.sync.dma_start(
+                out=tab_s[32 * q + PACK : 32 * q + PACK * (K_PASSES + 1), :].bitcast(I32),
+                in_=tab_scales[:, 4 * q : 4 * q + 4, :].bitcast(I32),
+            )
+
+        def load_w4_scales(q):
+            nc.sync.dma_start(
+                out=w4_raw_s[32 * q : 32 * q + 4, :, :].bitcast(I32),
+                in_=w4_scales[:, 4 * q : 4 * q + 4, :].rearrange("a r n -> r a n").bitcast(I32),
+            )
+
+        load_w1(0, 0)
+        nc.sync.dma_start(offs_sb[:], offs)
+        nc.sync.dma_start(out=gain_sb[:], in_=gain.rearrange("(b p t) -> p b t", p=P, t=PACK))
+        nc.sync.dma_start(pos1_sb[:], pos1)
+        load_tab(0)
+        load_w1(1, 0)
+        for q in range(4):
+            load_tab_scales(q)
+        nc.sync.dma_start(out=w4_raw[:].bitcast(I32), in_=w4_words.rearrange("a p n -> p a n").bitcast(I32))
+        load_tab(1)
+        load_w4_scales(0)
+        load_w4_scales(1)
+        load_w1(2, 0)
+        load_w4_scales(2)
+        load_w4_scales(3)
+        load_tab(2)
+        nc.sync.dma_start(pos2_sb[:], pos2)
+
+        for a in range(K_PASSES):
+            cast_w1(a, 0, 0)
+            if a == 0:
+                nc.scalar.copy(
+                    out=gain_rows[:],
+                    in_=gain_sb[:].rearrange("p b t -> p (b t)").unsqueeze(2).to_broadcast([P, BLOCKS * PACK, PAIRS]),
+                )
+                nc.vector.tensor_copy(v_s[:], tab_s[:].indirect(offs_sb[:]))
+            quantize_w1(a, 0)
+            if a == 1:
+                nc.vector.tensor_copy(
+                    out=w4_c[:].bitcast(U16).rearrange("p a (c t m) -> p (a c) m t", t=PACK, m=P),
+                    in_=w4_raw[:].bitcast(U16).rearrange("p a (c m t) -> p (a c) m t", t=PACK, m=P),
+                )
+                nc.vector.tensor_copy(
+                    out=w4_s[:].rearrange("p a (c t m) -> p (a c) m t", t=PACK, m=P),
+                    in_=w4_raw_s[:].rearrange("p a (c m t) -> p (a c) m t", t=PACK, m=P),
+                )
+            for u in range(HALVES):
+                gather_tab(a, u)
+                for t in range(PACK):
+                    first_pass(a, 0, t, u)
+        for a in range(K_PASSES):
+            load_w1(a, 1)
+        order = [(0, 0), (1, 0), (0, 1), (1, 1), (2, 0), (2, 1), (3, 0), (3, 1)]
+        for t, u in order:
+            square_h(0, t, u)
+
+        cast_w1(0, 1, P)
+        quantize_w1(0, 1)
+        cast_w1(1, 1, P)
+        quantize_w1(1, 1)
+        cast_w1(2, 1, 64)
+        quantize_w1(2, 1)
+        for t in range(PACK):
+            pick_x(0, t)
+        for a in range(K_PASSES):
+            for t in range(PACK):
+                for u in range(HALVES):
+                    first_pass(a, 1, t, u)
+        for t in range(PACK):
+            for u in range(HALVES):
+                square_h(1, t, u)
+            pick_x(1, t)
+        round_x(0, "scalar")
+        round_x(1, "vector")
+        quantize_x(0)
+        quantize_x(1)
+
+        out_rows = out.rearrange("(c p t) m -> c t p m", p=P, t=PACK)
+        y_sq, total = {}, {}
+
+        def second(c, t):
+            y = psum.tile([P, PAIRS], F32, name="bank")
+            col = c * SPAN + t * P
+            for b in range(BLOCKS):
+                nc.tensor.matmul_mx(
+                    out=y[:],
+                    lhsT=w4_c[:, b, 2 * col : 2 * (col + P)].bitcast(FP4X4),
+                    lhsT_scale=w4_s[:, b, col : col + P],
+                    rhs=x_c[b][:].bitcast(FP8X4),
+                    rhs_scale=x_s[b][:],
+                    start=(b == 0),
+                    stop=(b == BLOCKS - 1),
+                )
+            y_sq[c, t] = stage.tile([P, PAIRS], F32, name="y_sq", bufs=4)
+            nc.scalar.activation(out=y_sq[c, t][:], in_=y[:], func=ACT.Square)
+            total[c, t] = stage.tile([P, PAIRS], F32, name="total", bufs=4)
+            nc.vector.tensor_tensor(total[c, t][:], h[c, t][:].indirect(pos2_sb[:]), y_sq[c, t][:], ALU.add)
+
+        def finish(c, t):
+            res = stage.tile([P, PAIRS], F32, name="res")
+            nc.scalar.activation(out=res[:], in_=total[c, t][:], func=ACT.Sqrt, bias=eps[:])
+            nc.sync.dma_start(out=out_rows[c, t], in_=res[:])
+
+        tiles = [(c, t) for c in range(BLOCKS) for t in range(PACK)]
+        for i in range(len(tiles) + 2):
+            if i < len(tiles):
+                second(*tiles[i])
+            if i > 1:
+                finish(*tiles[i - 2])

@@ -22,7 +22,15 @@ SPAN = P * PACK
 K_PASSES = K // SPAN
 BLOCKS = H // SPAN
 HALVES = S // SPAN
-LIST_COLS = SPAN // 16
+QUADRANT = 32
+QUADRANTS = P // QUADRANT
+PER_COLUMN = 16
+MID = PAIRS // 2
+RUN = 4
+SQRT_LAG = 2
+
+LAST_CAST_ON_VECTOR = 32
+LAST_ROUNDING_ON_VECTOR = 76
 
 
 def tile_list_titanium_shock_pairs_kernel(
@@ -34,9 +42,9 @@ def tile_list_titanium_shock_pairs_kernel(
         stage = ctx.enter_context(tc.tile_pool(name="stage", bufs=3))
         psum = ctx.enter_context(tc.psum_pool(name="psum", bufs=8))
 
-        offs_sb = keep.tile([P, S // 16], U16, name="offs_sb")
-        pos1_sb = keep.tile([P, PAIRS // 16], U16, name="pos1_sb")
-        pos2_sb = keep.tile([P, PAIRS // 16], U16, name="pos2_sb")
+        offs_sb = keep.tile([P, S // PER_COLUMN], U16, name="offs_sb")
+        pos1_sb = keep.tile([P, PAIRS // PER_COLUMN], U16, name="pos1_sb")
+        pos2_sb = keep.tile([P, PAIRS // PER_COLUMN], U16, name="pos2_sb")
         tab_w = [keep.tile([P, T], I32, name="tab_w%d" % a) for a in range(K_PASSES)]
         tab_s = keep.tile([P, T], U8, name="tab_s")
         w4_raw = keep.tile([P, BLOCKS, 2 * H], U8, name="w4_raw")
@@ -44,12 +52,14 @@ def tile_list_titanium_shock_pairs_kernel(
         w4_c = keep.tile([P, BLOCKS, 2 * H], U8, name="w4_c", align_bytes=64)
         w4_s = keep.tile([P, BLOCKS, H], U8, name="w4_s", align_bytes=64)
         gain_sb = keep.tile([P, BLOCKS, PACK], F32, name="gain_sb")
-        gain_rows = keep.tile([P, BLOCKS * PACK, PAIRS], F32, name="gain_rows")
         eps = keep.tile([P, 1], F32, name="eps")
-        v_c = {}
         v_s = keep.tile([P, S], U8, name="v_s", align_bytes=64)
-        w_raw, w_bf, w_c, w_s = {}, {}, {}, {}
-        h, acc, x_f, x_bf, x_c, x_s = {}, {}, {}, {}, {}, {}
+        gain_row, v_c, w_raw, w_bf, w_c, w_s = {}, {}, {}, {}, {}, {}
+        h_sum, h, x_f, x_bf, x_c, x_s, y_sq, total = {}, {}, {}, {}, {}, {}, {}, {}
+
+        w_bf_tag = {(1, 1): "pass1", (2, 1): "pass2"}
+        x_f_tag = {(0, 0): "pass1", (0, MID): "pass2", (1, 0): "x_f_last"}
+        x_bf_tag = {(0, 0): "x_first", (0, MID): "squares", (1, 0): "x_last"}
 
         def load_w1(a, b):
             w_raw[a, b] = stage.tile([P, PACK, SPAN], F32, name="w_raw")
@@ -59,14 +69,17 @@ def tile_list_titanium_shock_pairs_kernel(
         def load_tab(a):
             nc.sync.dma_start(out=tab_w[a][:], in_=tab_words[a].rearrange("p t i -> p (t i)").bitcast(I32))
 
-        def cast_w1(a, b, m_vector):
-            w_bf[a, b] = stage.tile([P, PACK, P, PACK], BF16, name="w_bf", align_bytes=64)
+        def cast_w1(a, b, on_vector):
+            if (a, b) in w_bf_tag:
+                w_bf[a, b] = keep.tile([P, PACK, P, PACK], BF16, name="w_bf_late", tag=w_bf_tag[a, b], align_bytes=64)
+            else:
+                w_bf[a, b] = stage.tile([P, PACK, P, PACK], BF16, name="w_bf", bufs=2, align_bytes=64)
             dst = w_bf[a, b][:].rearrange("p t m j -> p m j t")
             src = w_raw[a, b][:].rearrange("p j (m t) -> p m j t", t=PACK)
-            if m_vector > 0:
-                nc.vector.tensor_copy(out=dst[:, :m_vector], in_=src[:, :m_vector])
-            if m_vector < P:
-                nc.scalar.copy(out=dst[:, m_vector:], in_=src[:, m_vector:])
+            if on_vector > 0:
+                nc.vector.tensor_copy(out=dst[:, :on_vector], in_=src[:, :on_vector])
+            if on_vector < P:
+                nc.scalar.copy(out=dst[:, on_vector:], in_=src[:, on_vector:])
 
         def quantize_w1(a, b):
             w_c[a, b] = keep.tile([P, SPAN], U32, name="w_c%d%d" % (a, b), align_bytes=64)
@@ -79,15 +92,15 @@ def tile_list_titanium_shock_pairs_kernel(
 
         def gather_tab(a, u):
             v_c[a, u] = keep.tile([P, SPAN], U32, name="v_c%d%d" % (a, u), align_bytes=64)
-            picks = offs_sb[:, u * LIST_COLS : (u + 1) * LIST_COLS]
-            nc.vector.tensor_copy(v_c[a, u][:], tab_w[a][:].bitcast(U32).indirect(picks))
+            entries = offs_sb[:, u * SPAN // PER_COLUMN : (u + 1) * SPAN // PER_COLUMN]
+            nc.vector.tensor_copy(v_c[a, u][:], tab_w[a][:].bitcast(U32).indirect(entries))
 
-        def first_pass(a, b, t, u):
+        def first_product(a, b, t, u):
             if a == 0:
-                acc[b, t, u] = psum.tile([P, SPAN], F32, name="bank")
+                h_sum[b, t, u] = psum.tile([P, SPAN], F32, name="bank")
             cols = slice(t * P, (t + 1) * P)
             nc.tensor.matmul_mx(
-                out=acc[b, t, u][:],
+                out=h_sum[b, t, u][:],
                 lhsT=w_c[a, b][:, cols].bitcast(FP8X4),
                 lhsT_scale=w_s[a, b][:, cols],
                 rhs=v_c[a, u][:].bitcast(FP8X4),
@@ -99,140 +112,165 @@ def tile_list_titanium_shock_pairs_kernel(
         def square_h(b, t, u):
             if u == 0:
                 h[b, t] = keep.tile([P, S], F32, name="h%d%d" % (b, t))
-            nc.scalar.activation(out=h[b, t][:, u * SPAN : (u + 1) * SPAN], in_=acc[b, t, u][:], func=ACT.Square)
-
-        def pick_x(b, t):
-            if t == 0:
-                x_f[b] = keep.tile([P, PACK, PAIRS], F32, name="x_f%d" % b)
-            nc.vector.tensor_tensor(
-                x_f[b][:, t, :], h[b, t][:].indirect(pos1_sb[:]), gain_rows[:, b * PACK + t, :], ALU.mult
+            nc.scalar.activation(
+                out=h[b, t][:, u * SPAN : (u + 1) * SPAN], in_=h_sum[b, t, u][:], func=ACT.Square, bias=zero[:]
             )
 
-        def round_x(b, engine):
-            x_bf[b] = keep.tile([P, PAIRS * PACK], BF16, name="x_bf%d" % b, align_bytes=64)
-            dst = x_bf[b][:].rearrange("p (c i t) -> p c t i", i=4, t=PACK)
-            src = x_f[b][:].rearrange("p t (c i) -> p c t i", i=4)
-            if engine == "vector":
-                nc.vector.tensor_copy(out=dst, in_=src)
-            else:
-                nc.scalar.copy(out=dst, in_=src)
+        def pick_x(b, t, m0, m1):
+            if t == 0:
+                x_f[b, m0] = keep.tile([P, PACK, m1 - m0], F32, name="x_f", tag=x_f_tag[b, m0], align_bytes=64)
+            nc.vector.tensor_tensor(
+                x_f[b, m0][:, t, :],
+                h[b, t][:].indirect(pos1_sb[:, m0 // PER_COLUMN : m1 // PER_COLUMN]),
+                gain_row[b, t][:, m0:m1],
+                ALU.mult,
+            )
 
-        def quantize_x(b):
-            x_c[b] = keep.tile([P, PAIRS], U32, name="x_c%d" % b, align_bytes=64)
-            x_s[b] = keep.tile([P, PAIRS], U8, name="x_s%d" % b, align_bytes=64)
-            nc.vector.quantize_mx(out=x_c[b][:].bitcast(FP8X4), scales=x_s[b][:], in_=x_bf[b][:])
+        def round_x(b, m0, m1, on_vector):
+            x_bf[b, m0] = keep.tile([P, (m1 - m0) * PACK], BF16, name="x_bf", tag=x_bf_tag[b, m0], align_bytes=64)
+            dst = x_bf[b, m0][:].rearrange("p (c i t) -> p c t i", i=RUN, t=PACK)
+            src = x_f[b, m0][:].rearrange("p t (c i) -> p c t i", i=RUN)
+            if on_vector > 0:
+                nc.vector.tensor_copy(out=dst[:, :on_vector], in_=src[:, :on_vector])
+            nc.scalar.copy(out=dst[:, on_vector:], in_=src[:, on_vector:])
+
+        def quantize_x(b, m0, m1):
+            if m0 == 0:
+                x_c[b] = keep.tile([P, PAIRS], U32, name="x_c%d" % b, align_bytes=64)
+                x_s[b] = keep.tile([P, PAIRS], U8, name="x_s%d" % b, align_bytes=64)
+            nc.vector.quantize_mx(out=x_c[b][:, m0:m1].bitcast(FP8X4), scales=x_s[b][:, m0:m1], in_=x_bf[b, m0][:])
 
         nc.vector.memset(tab_s[:].bitcast(I32), 0)
         nc.vector.memset(w4_raw_s[:].bitcast(I32), 0)
         nc.vector.memset(eps[:], 0.25)
-        def load_tab_scales(q):
-            nc.sync.dma_start(
-                out=tab_s[32 * q + PACK : 32 * q + PACK * (K_PASSES + 1), :].bitcast(I32),
-                in_=tab_scales[:, 4 * q : 4 * q + 4, :].bitcast(I32),
-            )
-
-        def load_w4_scales(q):
-            nc.sync.dma_start(
-                out=w4_raw_s[32 * q : 32 * q + 4, :, :].bitcast(I32),
-                in_=w4_scales[:, 4 * q : 4 * q + 4, :].rearrange("a r n -> r a n").bitcast(I32),
-            )
+        zero = keep.tile([P, 1], F32, name="zero", tag="squares", align_bytes=64)
+        nc.vector.memset(zero[:], 0.0)
+        warm = keep.tile([P, 1], F32, name="warm")
+        nc.scalar.activation(out=warm[:], in_=eps[:], func=ACT.Sqrt)
 
         load_w1(0, 0)
         nc.sync.dma_start(offs_sb[:], offs)
         nc.sync.dma_start(out=gain_sb[:], in_=gain.rearrange("(b p t) -> p b t", p=P, t=PACK))
-        nc.sync.dma_start(pos1_sb[:], pos1)
         load_tab(0)
         load_w1(1, 0)
-        for q in range(4):
-            load_tab_scales(q)
+        for q in range(QUADRANTS):
+            nc.gpsimd.dma_start(
+                out=tab_s[QUADRANT * q + PACK : QUADRANT * q + PACK * (K_PASSES + 1), :].bitcast(I32),
+                in_=tab_scales[:, PACK * q : PACK * (q + 1), :].bitcast(I32),
+            )
         nc.sync.dma_start(out=w4_raw[:].bitcast(I32), in_=w4_words.rearrange("a p n -> p a n").bitcast(I32))
         load_tab(1)
-        load_w4_scales(0)
-        load_w4_scales(1)
+        for q in range(QUADRANTS):
+            nc.gpsimd.dma_start(
+                out=w4_raw_s[QUADRANT * q : QUADRANT * q + PACK, :, :].bitcast(I32),
+                in_=w4_scales[:, PACK * q : PACK * (q + 1), :].rearrange("a r n -> r a n").bitcast(I32),
+            )
         load_w1(2, 0)
-        load_w4_scales(2)
-        load_w4_scales(3)
         load_tab(2)
+        nc.sync.dma_start(pos1_sb[:], pos1)
         nc.sync.dma_start(pos2_sb[:], pos2)
 
         for a in range(K_PASSES):
             cast_w1(a, 0, 0)
             if a == 0:
-                nc.scalar.copy(
-                    out=gain_rows[:],
-                    in_=gain_sb[:].rearrange("p b t -> p (b t)").unsqueeze(2).to_broadcast([P, BLOCKS * PACK, PAIRS]),
-                )
+                for b in range(BLOCKS):
+                    for t in range(PACK):
+                        gain_row[b, t] = keep.tile([P, PAIRS], F32, name="gain_row%d%d" % (b, t))
+                        nc.scalar.copy(out=gain_row[b, t][:], in_=gain_sb[:, b, t : t + 1].to_broadcast([P, PAIRS]))
                 nc.vector.tensor_copy(v_s[:], tab_s[:].indirect(offs_sb[:]))
             quantize_w1(a, 0)
             if a == 1:
                 nc.vector.tensor_copy(
-                    out=w4_c[:].bitcast(U16).rearrange("p a (c t m) -> p (a c) m t", t=PACK, m=P),
-                    in_=w4_raw[:].bitcast(U16).rearrange("p a (c m t) -> p (a c) m t", t=PACK, m=P),
+                    out=w4_c[:].bitcast(U16).rearrange("p a (c t m) -> p (a c) t m", t=PACK, m=P),
+                    in_=w4_raw[:].bitcast(U16).rearrange("p a (c m t) -> p (a c) t m", t=PACK, m=P),
                 )
                 nc.vector.tensor_copy(
-                    out=w4_s[:].rearrange("p a (c t m) -> p (a c) m t", t=PACK, m=P),
-                    in_=w4_raw_s[:].rearrange("p a (c m t) -> p (a c) m t", t=PACK, m=P),
+                    out=w4_s[:].rearrange("p a (c t m) -> p (a c) t m", t=PACK, m=P),
+                    in_=w4_raw_s[:].rearrange("p a (c m t) -> p (a c) t m", t=PACK, m=P),
                 )
             for u in range(HALVES):
                 gather_tab(a, u)
                 for t in range(PACK):
-                    first_pass(a, 0, t, u)
+                    first_product(a, 0, t, u)
         for a in range(K_PASSES):
             load_w1(a, 1)
-        order = [(0, 0), (1, 0), (0, 1), (1, 1), (2, 0), (2, 1), (3, 0), (3, 1)]
-        for t, u in order:
-            square_h(0, t, u)
+        for u in range(HALVES):
+            for t in range(PACK):
+                square_h(0, t, u)
 
         cast_w1(0, 1, P)
         quantize_w1(0, 1)
         cast_w1(1, 1, P)
         quantize_w1(1, 1)
-        cast_w1(2, 1, 64)
+        cast_w1(2, 1, LAST_CAST_ON_VECTOR)
+        for t in range(PACK):
+            pick_x(0, t, 0, MID)
         quantize_w1(2, 1)
         for t in range(PACK):
-            pick_x(0, t)
-        for a in range(K_PASSES):
+            pick_x(0, t, MID, PAIRS)
+        for u in range(HALVES):
+            for t in range(PACK):
+                first_product(0, 1, t, u)
+        for a in range(1, K_PASSES):
             for t in range(PACK):
                 for u in range(HALVES):
-                    first_pass(a, 1, t, u)
+                    first_product(a, 1, t, u)
         for t in range(PACK):
             for u in range(HALVES):
                 square_h(1, t, u)
-            pick_x(1, t)
-        round_x(0, "scalar")
-        round_x(1, "vector")
-        quantize_x(0)
-        quantize_x(1)
+            pick_x(1, t, 0, PAIRS)
+        round_x(0, 0, MID, 0)
+        round_x(0, MID, PAIRS, 0)
+        round_x(1, 0, PAIRS, LAST_ROUNDING_ON_VECTOR)
+        quantize_x(0, 0, MID)
+        quantize_x(0, MID, PAIRS)
+        quantize_x(1, 0, PAIRS)
+        first_pick = keep.tile([P, PAIRS], F32, name="first_pick", tag="x_last", align_bytes=64)
+        nc.vector.tensor_copy(first_pick[:], h[0, 0][:].indirect(pos2_sb[:]))
 
-        out_rows = out.rearrange("(c p t) m -> c t p m", p=P, t=PACK)
-        y_sq, total = {}, {}
+        out_rows = out.rearrange("(b p t) m -> b t p m", p=P, t=PACK)
+        row_tiles = [(b, t) for b in range(BLOCKS) for t in range(PACK)]
 
-        def second(c, t):
+        def pieces(b, t):
+            if (b, t) == row_tiles[-1]:
+                return [(0, MID), (MID, PAIRS)]
+            return [(0, PAIRS)]
+
+        def second_product(b, t):
             y = psum.tile([P, PAIRS], F32, name="bank")
-            col = c * SPAN + t * P
-            for b in range(BLOCKS):
+            col = b * SPAN + t * P
+            for a in range(BLOCKS):
                 nc.tensor.matmul_mx(
                     out=y[:],
-                    lhsT=w4_c[:, b, 2 * col : 2 * (col + P)].bitcast(FP4X4),
-                    lhsT_scale=w4_s[:, b, col : col + P],
-                    rhs=x_c[b][:].bitcast(FP8X4),
-                    rhs_scale=x_s[b][:],
-                    start=(b == 0),
-                    stop=(b == BLOCKS - 1),
+                    lhsT=w4_c[:, a, 2 * col : 2 * (col + P)].bitcast(FP4X4),
+                    lhsT_scale=w4_s[:, a, col : col + P],
+                    rhs=x_c[a][:].bitcast(FP8X4),
+                    rhs_scale=x_s[a][:],
+                    start=(a == 0),
+                    stop=(a == BLOCKS - 1),
                 )
-            y_sq[c, t] = stage.tile([P, PAIRS], F32, name="y_sq", bufs=4)
-            nc.scalar.activation(out=y_sq[c, t][:], in_=y[:], func=ACT.Square)
-            total[c, t] = stage.tile([P, PAIRS], F32, name="total", bufs=4)
-            nc.vector.tensor_tensor(total[c, t][:], h[c, t][:].indirect(pos2_sb[:]), y_sq[c, t][:], ALU.add)
+            y_sq[b, t] = stage.tile([P, PAIRS], F32, name="y_sq", bufs=SQRT_LAG + 2)
+            nc.scalar.activation(out=y_sq[b, t][:], in_=y[:], func=ACT.Square)
+            total[b, t] = stage.tile([P, PAIRS], F32, name="total", bufs=len(row_tiles))
+            if (b, t) == row_tiles[0]:
+                nc.vector.tensor_tensor(total[b, t][:], first_pick[:], y_sq[b, t][:], ALU.add)
+            else:
+                for m0, m1 in pieces(b, t):
+                    nc.vector.tensor_tensor(
+                        total[b, t][:, m0:m1],
+                        h[b, t][:].indirect(pos2_sb[:, m0 // PER_COLUMN : m1 // PER_COLUMN]),
+                        y_sq[b, t][:, m0:m1],
+                        ALU.add,
+                    )
 
-        def finish(c, t):
-            res = stage.tile([P, PAIRS], F32, name="res")
-            nc.scalar.activation(out=res[:], in_=total[c, t][:], func=ACT.Sqrt, bias=eps[:])
-            nc.sync.dma_start(out=out_rows[c, t], in_=res[:])
+        def finish(b, t):
+            for m0, m1 in pieces(b, t):
+                part = total[b, t][:, m0:m1]
+                nc.scalar.activation(out=part, in_=part, func=ACT.Sqrt, bias=eps[:])
+                nc.sync.dma_start(out=out_rows[b, t][:, m0:m1], in_=part)
 
-        tiles = [(c, t) for c in range(BLOCKS) for t in range(PACK)]
-        for i in range(len(tiles) + 2):
-            if i < len(tiles):
-                second(*tiles[i])
-            if i > 1:
-                finish(*tiles[i - 2])
+        for i in range(len(row_tiles) + SQRT_LAG):
+            if i < len(row_tiles):
+                second_product(*row_tiles[i])
+            if i >= SQRT_LAG:
+                finish(*row_tiles[i - SQRT_LAG])

@@ -29,8 +29,12 @@ MID = PAIRS // 2
 RUN = 4
 SQRT_LAG = 2
 
-LAST_CAST_ON_VECTOR = 32
-LAST_ROUNDING_ON_VECTOR = 76
+MIDDLE_CAST_ON_VECTOR = 76
+LAST_CAST_ON_VECTOR = 40
+
+TAB_BYTES = 4 * T
+W_BYTES = 4 * PACK * SPAN
+W_AREA = K_PASSES * TAB_BYTES
 
 
 def tile_list_titanium_shock_pairs_kernel(
@@ -39,56 +43,70 @@ def tile_list_titanium_shock_pairs_kernel(
     nc = tc.nc
     with ExitStack() as ctx:
         keep = ctx.enter_context(tc.tile_pool(name="keep", bufs=1))
-        stage = ctx.enter_context(tc.tile_pool(name="stage", bufs=3))
+        areas = ctx.enter_context(tc.tile_pool(name="areas", bufs=1))
+        stage = ctx.enter_context(tc.tile_pool(name="stage", bufs=2))
         psum = ctx.enter_context(tc.psum_pool(name="psum", bufs=8))
 
         offs_sb = keep.tile([P, S // PER_COLUMN], U16, name="offs_sb")
         pos1_sb = keep.tile([P, PAIRS // PER_COLUMN], U16, name="pos1_sb")
         pos2_sb = keep.tile([P, PAIRS // PER_COLUMN], U16, name="pos2_sb")
-        tab_w = [keep.tile([P, T], I32, name="tab_w%d" % a) for a in range(K_PASSES)]
         tab_s = keep.tile([P, T], U8, name="tab_s")
-        w4_raw = keep.tile([P, BLOCKS, 2 * H], U8, name="w4_raw")
         w4_raw_s = keep.tile([P, BLOCKS, H], U8, name="w4_raw_s")
         w4_c = keep.tile([P, BLOCKS, 2 * H], U8, name="w4_c", align_bytes=64)
         w4_s = keep.tile([P, BLOCKS, H], U8, name="w4_s", align_bytes=64)
         gain_sb = keep.tile([P, BLOCKS, PACK], F32, name="gain_sb")
         eps = keep.tile([P, 1], F32, name="eps")
         v_s = keep.tile([P, S], U8, name="v_s", align_bytes=64)
-        gain_row, v_c, w_raw, w_bf, w_c, w_s = {}, {}, {}, {}, {}, {}
-        h_sum, h, x_f, x_bf, x_c, x_s, y_sq, total = {}, {}, {}, {}, {}, {}, {}, {}
+        x_f0 = keep.tile([P, PACK * 2 * PAIRS], F32, name="x_f0", align_bytes=64)
+        x_f1 = keep.tile([P, PACK * PAIRS], F32, name="x_f1", align_bytes=64)
+        x_f = [
+            x_f0[:].rearrange("p (t m) -> p t m", t=PACK)[:, :, :PAIRS],
+            x_f1[:].rearrange("p (t m) -> p t m", t=PACK),
+        ]
+        tab_w, gain_row, v_c, w_raw, w_bf, w_c, w_s = {}, {}, {}, {}, {}, {}, {}
+        h_sum, h, x_bf, x_c, x_s, y_sq, total = {}, {}, {}, {}, {}, {}, {}
 
-        w_bf_tag = {(1, 1): "pass1", (2, 1): "pass2"}
-        x_f_tag = {(0, 0): "pass1", (0, MID): "pass2", (1, 0): "x_f_last"}
-        x_bf_tag = {(0, 0): "x_first", (0, MID): "squares", (1, 0): "x_last"}
-
-        def load_w1(a, b):
-            w_raw[a, b] = stage.tile([P, PACK, SPAN], F32, name="w_raw")
+        def load_w1(a, b, offset):
+            w_raw[a, b] = areas.tile([P, PACK, SPAN], F32, name="w_raw%d%d" % (a, b), offset=offset)
             rows = w1[a * SPAN : (a + 1) * SPAN, b * SPAN : (b + 1) * SPAN]
             nc.sync.dma_start(out=w_raw[a, b][:], in_=rows.rearrange("(p j) c -> p j c", j=PACK))
 
         def load_tab(a):
+            tab_w[a] = areas.tile([P, T], I32, name="tab_w%d" % a, offset=a * TAB_BYTES)
             nc.sync.dma_start(out=tab_w[a][:], in_=tab_words[a].rearrange("p t i -> p (t i)").bitcast(I32))
 
-        def cast_w1(a, b, on_vector):
-            if (a, b) in w_bf_tag:
-                w_bf[a, b] = keep.tile([P, PACK, P, PACK], BF16, name="w_bf_late", tag=w_bf_tag[a, b], align_bytes=64)
+        def cast_views(a, b):
+            if a > 0 and b == 1:
+                w_bf[a, b] = x_f0[:, (a + 1) * 2 * PAIRS : (a + 2) * 2 * PAIRS].bitcast(BF16)
             else:
-                w_bf[a, b] = stage.tile([P, PACK, P, PACK], BF16, name="w_bf", bufs=2, align_bytes=64)
-            dst = w_bf[a, b][:].rearrange("p t m j -> p m j t")
+                w_bf[a, b] = stage.tile([P, PACK * SPAN], BF16, name="w_bf", align_bytes=64)[:]
+            dst = w_bf[a, b].rearrange("p (t m j) -> p m j t", t=PACK, j=PACK)
             src = w_raw[a, b][:].rearrange("p j (m t) -> p m j t", t=PACK)
+            return dst, src
+
+        def cast_w1(a, b, on_vector):
+            dst, src = cast_views(a, b)
             if on_vector > 0:
                 nc.vector.tensor_copy(out=dst[:, :on_vector], in_=src[:, :on_vector])
             if on_vector < P:
                 nc.scalar.copy(out=dst[:, on_vector:], in_=src[:, on_vector:])
 
-        def quantize_w1(a, b):
-            w_c[a, b] = keep.tile([P, SPAN], U32, name="w_c%d%d" % (a, b), align_bytes=64)
+        def cast_w1_by_tiles(a, b):
+            dst, src = cast_views(a, b)
+            nc.vector.tensor_copy(out=dst[:, :, :, :2], in_=src[:, :, :, :2])
+            nc.scalar.copy(out=dst[:, :, :, 2:], in_=src[:, :, :, 2:])
+
+        def quantize_w1(a, b, parts):
+            tag = "x_bf0" if (a, b) == (K_PASSES - 1, BLOCKS - 1) else "w_c%d%d" % (a, b)
+            w_c[a, b] = keep.tile([P, SPAN], U32, name="w_c", tag=tag, align_bytes=64)
             w_s[a, b] = keep.tile([P, SPAN], U8, name="w_s%d%d" % (a, b), align_bytes=64)
-            nc.vector.quantize_mx(
-                out=w_c[a, b][:].bitcast(FP8X4),
-                scales=w_s[a, b][:],
-                in_=w_bf[a, b][:].rearrange("p t m j -> p (t m j)"),
-            )
+            width = SPAN // parts
+            for c in range(0, SPAN, width):
+                nc.vector.quantize_mx(
+                    out=w_c[a, b][:, c : c + width].bitcast(FP8X4),
+                    scales=w_s[a, b][:, c : c + width],
+                    in_=w_bf[a, b][:, PACK * c : PACK * (c + width)],
+                )
 
         def gather_tab(a, u):
             v_c[a, u] = keep.tile([P, SPAN], U32, name="v_c%d%d" % (a, u), align_bytes=64)
@@ -109,123 +127,123 @@ def tile_list_titanium_shock_pairs_kernel(
                 stop=(a == K_PASSES - 1),
             )
 
-        def square_h(b, t, u):
-            if u == 0:
-                h[b, t] = keep.tile([P, S], F32, name="h%d%d" % (b, t))
-            nc.scalar.activation(
-                out=h[b, t][:, u * SPAN : (u + 1) * SPAN], in_=h_sum[b, t, u][:], func=ACT.Square, bias=zero[:]
-            )
+        def square_h(b, t):
+            h[b, t] = keep.tile([P, S], F32, name="h%d%d" % (b, t))
+            for u in range(HALVES):
+                nc.scalar.activation(out=h[b, t][:, u * SPAN : (u + 1) * SPAN], in_=h_sum[b, t, u][:], func=ACT.Square)
 
-        def pick_x(b, t, m0, m1):
-            if t == 0:
-                x_f[b, m0] = keep.tile([P, PACK, m1 - m0], F32, name="x_f", tag=x_f_tag[b, m0], align_bytes=64)
+        def pick_x(b, t):
             nc.vector.tensor_tensor(
-                x_f[b, m0][:, t, :],
-                h[b, t][:].indirect(pos1_sb[:, m0 // PER_COLUMN : m1 // PER_COLUMN]),
-                gain_row[b, t][:, m0:m1],
-                ALU.mult,
+                x_f[b][:, t, :], h[b, t][:].indirect(pos1_sb[:]), gain_row[b, t][:], ALU.mult
             )
 
-        def round_x(b, m0, m1, on_vector):
-            x_bf[b, m0] = keep.tile([P, (m1 - m0) * PACK], BF16, name="x_bf", tag=x_bf_tag[b, m0], align_bytes=64)
-            dst = x_bf[b, m0][:].rearrange("p (c i t) -> p c t i", i=RUN, t=PACK)
-            src = x_f[b, m0][:].rearrange("p t (c i) -> p c t i", i=RUN)
-            if on_vector > 0:
-                nc.vector.tensor_copy(out=dst[:, :on_vector], in_=src[:, :on_vector])
-            nc.scalar.copy(out=dst[:, on_vector:], in_=src[:, on_vector:])
+        def round_x(b, on_vector):
+            x_bf[b] = keep.tile([P, PAIRS * PACK], BF16, name="x_bf", tag="x_bf%d" % b, align_bytes=64)
+            dst = x_bf[b][:].rearrange("p (c i t) -> p c t i", i=RUN, t=PACK)
+            src = x_f[b].rearrange("p t (c i) -> p c t i", i=RUN)
+            if on_vector:
+                nc.vector.tensor_copy(out=dst, in_=src)
+            else:
+                nc.scalar.copy(out=dst, in_=src)
 
-        def quantize_x(b, m0, m1):
-            if m0 == 0:
-                x_c[b] = keep.tile([P, PAIRS], U32, name="x_c%d" % b, align_bytes=64)
-                x_s[b] = keep.tile([P, PAIRS], U8, name="x_s%d" % b, align_bytes=64)
-            nc.vector.quantize_mx(out=x_c[b][:, m0:m1].bitcast(FP8X4), scales=x_s[b][:, m0:m1], in_=x_bf[b, m0][:])
+        def quantize_x(b):
+            x_c[b] = keep.tile([P, PAIRS], U32, name="x_c%d" % b, align_bytes=64)
+            x_s[b] = keep.tile([P, PAIRS], U8, name="x_s%d" % b, align_bytes=64)
+            nc.vector.quantize_mx(out=x_c[b][:].bitcast(FP8X4), scales=x_s[b][:], in_=x_bf[b][:])
 
         nc.vector.memset(tab_s[:].bitcast(I32), 0)
         nc.vector.memset(w4_raw_s[:].bitcast(I32), 0)
         nc.vector.memset(eps[:], 0.25)
-        zero = keep.tile([P, 1], F32, name="zero", tag="squares", align_bytes=64)
-        nc.vector.memset(zero[:], 0.0)
         warm = keep.tile([P, 1], F32, name="warm")
         nc.scalar.activation(out=warm[:], in_=eps[:], func=ACT.Sqrt)
 
-        load_w1(0, 0)
+        load_w1(0, 0, W_AREA)
         nc.sync.dma_start(offs_sb[:], offs)
-        nc.sync.dma_start(out=gain_sb[:], in_=gain.rearrange("(b p t) -> p b t", p=P, t=PACK))
         load_tab(0)
-        load_w1(1, 0)
+        nc.sync.dma_start(out=gain_sb[:], in_=gain.rearrange("(b p t) -> p b t", p=P, t=PACK))
         for q in range(QUADRANTS):
             nc.gpsimd.dma_start(
                 out=tab_s[QUADRANT * q + PACK : QUADRANT * q + PACK * (K_PASSES + 1), :].bitcast(I32),
                 in_=tab_scales[:, PACK * q : PACK * (q + 1), :].bitcast(I32),
             )
-        nc.sync.dma_start(out=w4_raw[:].bitcast(I32), in_=w4_words.rearrange("a p n -> p a n").bitcast(I32))
         load_tab(1)
+        nc.sync.dma_start(pos1_sb[:], pos1)
+        nc.sync.dma_start(pos2_sb[:], pos2)
         for q in range(QUADRANTS):
-            nc.gpsimd.dma_start(
+            nc.sync.dma_start(
                 out=w4_raw_s[QUADRANT * q : QUADRANT * q + PACK, :, :].bitcast(I32),
                 in_=w4_scales[:, PACK * q : PACK * (q + 1), :].rearrange("a r n -> r a n").bitcast(I32),
             )
-        load_w1(2, 0)
-        load_tab(2)
-        nc.sync.dma_start(pos1_sb[:], pos1)
-        nc.sync.dma_start(pos2_sb[:], pos2)
 
-        for a in range(K_PASSES):
-            cast_w1(a, 0, 0)
-            if a == 0:
-                for b in range(BLOCKS):
-                    for t in range(PACK):
-                        gain_row[b, t] = keep.tile([P, PAIRS], F32, name="gain_row%d%d" % (b, t))
-                        nc.scalar.copy(out=gain_row[b, t][:], in_=gain_sb[:, b, t : t + 1].to_broadcast([P, PAIRS]))
-                nc.vector.tensor_copy(v_s[:], tab_s[:].indirect(offs_sb[:]))
-            quantize_w1(a, 0)
-            if a == 1:
-                nc.vector.tensor_copy(
-                    out=w4_c[:].bitcast(U16).rearrange("p a (c t m) -> p (a c) t m", t=PACK, m=P),
-                    in_=w4_raw[:].bitcast(U16).rearrange("p a (c m t) -> p (a c) t m", t=PACK, m=P),
-                )
-                nc.vector.tensor_copy(
-                    out=w4_s[:].rearrange("p a (c t m) -> p (a c) t m", t=PACK, m=P),
-                    in_=w4_raw_s[:].rearrange("p a (c m t) -> p (a c) t m", t=PACK, m=P),
-                )
-            for u in range(HALVES):
-                gather_tab(a, u)
-                for t in range(PACK):
-                    first_product(a, 0, t, u)
-        for a in range(K_PASSES):
-            load_w1(a, 1)
+        cast_w1(0, 0, 0)
+        load_w1(1, 0, W_AREA + W_BYTES)
+        for b in range(BLOCKS):
+            for t in range(PACK):
+                gain_row[b, t] = keep.tile([P, PAIRS], F32, name="gain_row%d%d" % (b, t))
+                nc.scalar.copy(out=gain_row[b, t][:], in_=gain_sb[:, b, t : t + 1].to_broadcast([P, PAIRS]))
+        quantize_w1(0, 0, 1)
+        nc.vector.tensor_copy(v_s[:], tab_s[:].indirect(offs_sb[:]))
+        for u in range(HALVES):
+            gather_tab(0, u)
+            for t in range(PACK):
+                first_product(0, 0, t, u)
+        w4_raw = keep.tile([P, BLOCKS, 2 * H], U8, name="w4_raw")
+        nc.sync.dma_start(out=w4_raw[:].bitcast(I32), in_=w4_words.rearrange("a p n -> p a n").bitcast(I32))
+        load_tab(2)
+        for u in range(HALVES):
+            gather_tab(1, u)
+        load_w1(2, 0, W_AREA + 2 * W_BYTES)
+        nc.vector.tensor_copy(
+            out=w4_s[:].rearrange("p a (c t m) -> p (a c) t m", t=PACK, m=P),
+            in_=w4_raw_s[:].rearrange("p a (c m t) -> p (a c) t m", t=PACK, m=P),
+        )
+        nc.vector.tensor_copy(
+            out=w4_c[:].bitcast(U16).rearrange("p a (c t m) -> p (a c) t m", t=PACK, m=P),
+            in_=w4_raw[:].bitcast(U16).rearrange("p a (c m t) -> p (a c) t m", t=PACK, m=P),
+        )
+        cast_w1(1, 0, 0)
+        load_w1(0, 1, W_AREA)
+        quantize_w1(1, 0, 1)
         for u in range(HALVES):
             for t in range(PACK):
-                square_h(0, t, u)
+                first_product(1, 0, t, u)
+        for u in range(HALVES):
+            gather_tab(2, u)
+        load_w1(1, 1, 0)
+        load_w1(2, 1, W_BYTES)
+        cast_w1_by_tiles(2, 0)
+        quantize_w1(2, 0, 2)
+        for t in range(PACK):
+            for u in range(HALVES):
+                first_product(2, 0, t, u)
+        for t in range(PACK):
+            square_h(0, t)
 
         cast_w1(0, 1, P)
-        quantize_w1(0, 1)
-        cast_w1(1, 1, P)
-        quantize_w1(1, 1)
+        pick_x(0, 0)
+        quantize_w1(0, 1, 1)
+        cast_w1(1, 1, MIDDLE_CAST_ON_VECTOR)
+        pick_x(0, 1)
+        quantize_w1(1, 1, 1)
         cast_w1(2, 1, LAST_CAST_ON_VECTOR)
+        pick_x(0, 2)
+        quantize_w1(2, 1, 1)
+        pick_x(0, 3)
         for t in range(PACK):
-            pick_x(0, t, 0, MID)
-        quantize_w1(2, 1)
-        for t in range(PACK):
-            pick_x(0, t, MID, PAIRS)
-        for u in range(HALVES):
-            for t in range(PACK):
+            for u in range(HALVES):
                 first_product(0, 1, t, u)
-        for a in range(1, K_PASSES):
-            for t in range(PACK):
+        for t in range(PACK):
+            for a in range(1, K_PASSES):
                 for u in range(HALVES):
                     first_product(a, 1, t, u)
         for t in range(PACK):
-            for u in range(HALVES):
-                square_h(1, t, u)
-            pick_x(1, t, 0, PAIRS)
-        round_x(0, 0, MID, 0)
-        round_x(0, MID, PAIRS, 0)
-        round_x(1, 0, PAIRS, LAST_ROUNDING_ON_VECTOR)
-        quantize_x(0, 0, MID)
-        quantize_x(0, MID, PAIRS)
-        quantize_x(1, 0, PAIRS)
-        first_pick = keep.tile([P, PAIRS], F32, name="first_pick", tag="x_last", align_bytes=64)
+            square_h(1, t)
+            pick_x(1, t)
+        round_x(0, False)
+        round_x(1, True)
+        quantize_x(1)
+        quantize_x(0)
+        first_pick = keep.tile([P, PAIRS], F32, name="first_pick", tag="x_bf0", align_bytes=64)
         nc.vector.tensor_copy(first_pick[:], h[0, 0][:].indirect(pos2_sb[:]))
 
         out_rows = out.rearrange("(b p t) m -> b t p m", p=P, t=PACK)
@@ -239,19 +257,20 @@ def tile_list_titanium_shock_pairs_kernel(
         def second_product(b, t):
             y = psum.tile([P, PAIRS], F32, name="bank")
             col = b * SPAN + t * P
-            for a in range(BLOCKS):
+            for a in reversed(range(BLOCKS)):
                 nc.tensor.matmul_mx(
                     out=y[:],
                     lhsT=w4_c[:, a, 2 * col : 2 * (col + P)].bitcast(FP4X4),
                     lhsT_scale=w4_s[:, a, col : col + P],
                     rhs=x_c[a][:].bitcast(FP8X4),
                     rhs_scale=x_s[a][:],
-                    start=(a == 0),
-                    stop=(a == BLOCKS - 1),
+                    start=(a == BLOCKS - 1),
+                    stop=(a == 0),
                 )
             y_sq[b, t] = stage.tile([P, PAIRS], F32, name="y_sq", bufs=SQRT_LAG + 2)
             nc.scalar.activation(out=y_sq[b, t][:], in_=y[:], func=ACT.Square)
-            total[b, t] = stage.tile([P, PAIRS], F32, name="total", bufs=len(row_tiles))
+            offset = TAB_BYTES + 4 * PAIRS * (PACK * b + t)
+            total[b, t] = areas.tile([P, PAIRS], F32, name="total%d%d" % (b, t), offset=offset)
             if (b, t) == row_tiles[0]:
                 nc.vector.tensor_tensor(total[b, t][:], first_pick[:], y_sq[b, t][:], ALU.add)
             else:

@@ -56,7 +56,6 @@ def tile_list_titanium_shock_pairs_kernel(
         w4_s = keep.tile([P, BLOCKS, H], U8, name="w4_s", align_bytes=64)
         gain_sb = keep.tile([P, BLOCKS, PACK], F32, name="gain_sb")
         eps = keep.tile([P, 1], F32, name="eps")
-        v_s = keep.tile([P, S], U8, name="v_s", align_bytes=64)
         x_f0 = keep.tile([P, PACK * 2 * PAIRS], F32, name="x_f0", align_bytes=64)
         x_f1 = keep.tile([P, PACK * PAIRS], F32, name="x_f1", align_bytes=64)
         x_f = [
@@ -182,16 +181,18 @@ def tile_list_titanium_shock_pairs_kernel(
                 gain_row[b, t] = keep.tile([P, PAIRS], F32, name="gain_row%d%d" % (b, t))
                 nc.scalar.copy(out=gain_row[b, t][:], in_=gain_sb[:, b, t : t + 1].to_broadcast([P, PAIRS]))
         quantize_w1(0, 0, 1)
-        nc.vector.tensor_copy(v_s[:], tab_s[:].indirect(offs_sb[:]))
         for u in range(HALVES):
             gather_tab(0, u)
-            for t in range(PACK):
-                first_product(0, 0, t, u)
         w4_raw = keep.tile([P, BLOCKS, 2 * H], U8, name="w4_raw")
         nc.sync.dma_start(out=w4_raw[:].bitcast(I32), in_=w4_words.rearrange("a p n -> p a n").bitcast(I32))
         load_tab(2)
         for u in range(HALVES):
             gather_tab(1, u)
+        v_s = areas.tile([P, S], U8, name="v_s", offset=TAB_BYTES, align_bytes=64)
+        nc.vector.tensor_copy(v_s[:], tab_s[:].indirect(offs_sb[:]))
+        for u in range(HALVES):
+            for t in range(PACK):
+                first_product(0, 0, t, u)
         load_w1(2, 0, W_AREA + 2 * W_BYTES)
         nc.vector.tensor_copy(
             out=w4_s[:].rearrange("p a (c t m) -> p (a c) t m", t=PACK, m=P),
@@ -269,7 +270,7 @@ def tile_list_titanium_shock_pairs_kernel(
                 )
             y_sq[b, t] = stage.tile([P, PAIRS], F32, name="y_sq", bufs=SQRT_LAG + 2)
             nc.scalar.activation(out=y_sq[b, t][:], in_=y[:], func=ACT.Square)
-            offset = TAB_BYTES + 4 * PAIRS * (PACK * b + t)
+            offset = 2 * TAB_BYTES + 4 * PAIRS * (PACK * b + t)
             total[b, t] = areas.tile([P, PAIRS], F32, name="total%d%d" % (b, t), offset=offset)
             if (b, t) == row_tiles[0]:
                 nc.vector.tensor_tensor(total[b, t][:], first_pick[:], y_sq[b, t][:], ALU.add)

@@ -29,8 +29,7 @@ MID = PAIRS // 2
 RUN = 4
 SQRT_LAG = 2
 
-MIDDLE_CAST_ON_VECTOR = 76
-LAST_CAST_ON_VECTOR = 40
+LAST_CAST_ON_VECTOR = 80
 
 TAB_BYTES = 4 * T
 W_BYTES = 4 * PACK * SPAN
@@ -56,10 +55,11 @@ def tile_list_titanium_shock_pairs_kernel(
         w4_s = keep.tile([P, BLOCKS, H], U8, name="w4_s", align_bytes=64)
         gain_sb = keep.tile([P, BLOCKS, PACK], F32, name="gain_sb")
         eps = keep.tile([P, 1], F32, name="eps")
-        x_f0 = keep.tile([P, PACK * 2 * PAIRS], F32, name="x_f0", align_bytes=64)
+        x_f0 = keep.tile([P, (PACK - 1) * PAIRS + PACK * SPAN], F32, name="x_f0", align_bytes=64)
+        late_bf = x_f0[:, (PACK - 1) * PAIRS :].bitcast(BF16)
         x_f1 = keep.tile([P, PACK * PAIRS], F32, name="x_f1", align_bytes=64)
         x_f = [
-            x_f0[:].rearrange("p (t m) -> p t m", t=PACK)[:, :, :PAIRS],
+            x_f0[:, : PACK * PAIRS].rearrange("p (t m) -> p t m", t=PACK),
             x_f1[:].rearrange("p (t m) -> p t m", t=PACK),
         ]
         tab_w, gain_row, v_c, w_raw, w_bf, w_c, w_s = {}, {}, {}, {}, {}, {}, {}
@@ -76,10 +76,10 @@ def tile_list_titanium_shock_pairs_kernel(
 
         def cast_views(a, b):
             if a > 0 and b == 1:
-                w_bf[a, b] = x_f0[:, (a + 1) * 2 * PAIRS : (a + 2) * 2 * PAIRS].bitcast(BF16)
+                dst = late_bf.rearrange("p (t a m j) -> p a m j t", t=PACK, a=2, j=PACK)[:, a - 1]
             else:
                 w_bf[a, b] = stage.tile([P, PACK * SPAN], BF16, name="w_bf", align_bytes=64)[:]
-            dst = w_bf[a, b].rearrange("p (t m j) -> p m j t", t=PACK, j=PACK)
+                dst = w_bf[a, b].rearrange("p (t m j) -> p m j t", t=PACK, j=PACK)
             src = w_raw[a, b][:].rearrange("p j (m t) -> p m j t", t=PACK)
             return dst, src
 
@@ -95,17 +95,31 @@ def tile_list_titanium_shock_pairs_kernel(
             nc.vector.tensor_copy(out=dst[:, :, :, :2], in_=src[:, :, :, :2])
             nc.scalar.copy(out=dst[:, :, :, 2:], in_=src[:, :, :, 2:])
 
-        def quantize_w1(a, b, parts):
-            tag = "x_bf0" if (a, b) == (K_PASSES - 1, BLOCKS - 1) else "w_c%d%d" % (a, b)
-            w_c[a, b] = keep.tile([P, SPAN], U32, name="w_c", tag=tag, align_bytes=64)
-            w_s[a, b] = keep.tile([P, SPAN], U8, name="w_s%d%d" % (a, b), align_bytes=64)
-            width = SPAN // parts
-            for c in range(0, SPAN, width):
+        def quantize(codes, scales, values, width):
+            for c in range(0, codes.shape[1], width):
                 nc.vector.quantize_mx(
-                    out=w_c[a, b][:, c : c + width].bitcast(FP8X4),
-                    scales=w_s[a, b][:, c : c + width],
-                    in_=w_bf[a, b][:, PACK * c : PACK * (c + width)],
+                    out=codes[:, c : c + width].bitcast(FP8X4),
+                    scales=scales[:, c : c + width],
+                    in_=values[:, PACK * c : PACK * (c + width)],
                 )
+
+        def quantize_w1(a, b, parts):
+            codes = keep.tile([P, SPAN], U32, name="w_c%d%d" % (a, b), align_bytes=64)
+            scales = keep.tile([P, SPAN], U8, name="w_s%d%d" % (a, b), align_bytes=64)
+            quantize(codes, scales, w_bf[a, b], SPAN // parts)
+            for t in range(PACK):
+                w_c[a, b, t] = codes[:, t * P : (t + 1) * P]
+                w_s[a, b, t] = scales[:, t * P : (t + 1) * P]
+
+        def quantize_late():
+            codes = keep.tile([P, 2 * SPAN], U32, name="late_c", tag="x_bf0", align_bytes=64)
+            scales = keep.tile([P, 2 * SPAN], U8, name="late_s", align_bytes=64)
+            quantize(codes, scales, late_bf, SPAN)
+            for t in range(PACK):
+                for a in (1, 2):
+                    cols = slice((2 * t + a - 1) * P, (2 * t + a) * P)
+                    w_c[a, 1, t] = codes[:, cols]
+                    w_s[a, 1, t] = scales[:, cols]
 
         def gather_tab(a, u):
             v_c[a, u] = keep.tile([P, SPAN], U32, name="v_c%d%d" % (a, u), align_bytes=64)
@@ -115,11 +129,10 @@ def tile_list_titanium_shock_pairs_kernel(
         def first_product(a, b, t, u):
             if a == 0:
                 h_sum[b, t, u] = psum.tile([P, SPAN], F32, name="bank")
-            cols = slice(t * P, (t + 1) * P)
             nc.tensor.matmul_mx(
                 out=h_sum[b, t, u][:],
-                lhsT=w_c[a, b][:, cols].bitcast(FP8X4),
-                lhsT_scale=w_s[a, b][:, cols],
+                lhsT=w_c[a, b, t].bitcast(FP8X4),
+                lhsT_scale=w_s[a, b, t],
                 rhs=v_c[a, u][:].bitcast(FP8X4),
                 rhs_scale=v_s[PACK * (a + 1) :, u * SPAN : (u + 1) * SPAN],
                 start=(a == 0),
@@ -131,9 +144,10 @@ def tile_list_titanium_shock_pairs_kernel(
             for u in range(HALVES):
                 nc.scalar.activation(out=h[b, t][:, u * SPAN : (u + 1) * SPAN], in_=h_sum[b, t, u][:], func=ACT.Square)
 
-        def pick_x(b, t):
+        def pick_x(b, t, m0=0, m1=PAIRS):
+            entries = pos1_sb[:, m0 // PER_COLUMN : m1 // PER_COLUMN]
             nc.vector.tensor_tensor(
-                x_f[b][:, t, :], h[b, t][:].indirect(pos1_sb[:]), gain_row[b, t][:], ALU.mult
+                x_f[b][:, t, m0:m1], h[b, t][:].indirect(entries), gain_row[b, t][:, m0:m1], ALU.mult
             )
 
         def round_x(b, on_vector):
@@ -141,17 +155,19 @@ def tile_list_titanium_shock_pairs_kernel(
             dst = x_bf[b][:].rearrange("p (c i t) -> p c t i", i=RUN, t=PACK)
             src = x_f[b].rearrange("p t (c i) -> p c t i", i=RUN)
             if on_vector:
-                nc.vector.tensor_copy(out=dst, in_=src)
+                nc.vector.tensor_copy(out=dst[:, : MID // RUN], in_=src[:, : MID // RUN])
+                nc.vector.tensor_copy(out=dst[:, MID // RUN :], in_=src[:, MID // RUN :])
             else:
                 nc.scalar.copy(out=dst, in_=src)
 
-        def quantize_x(b):
-            x_c[b] = keep.tile([P, PAIRS], U32, name="x_c%d" % b, align_bytes=64)
-            x_s[b] = keep.tile([P, PAIRS], U8, name="x_s%d" % b, align_bytes=64)
-            nc.vector.quantize_mx(out=x_c[b][:].bitcast(FP8X4), scales=x_s[b][:], in_=x_bf[b][:])
+        def quantize_x(b, m0, m1):
+            if m0 == 0:
+                x_c[b] = keep.tile([P, PAIRS], U32, name="x_c%d" % b, align_bytes=64)
+                x_s[b] = keep.tile([P, PAIRS], U8, name="x_s%d" % b, align_bytes=64)
+            quantize(x_c[b][:, m0:m1], x_s[b][:, m0:m1], x_bf[b][:, PACK * m0 : PACK * m1], m1 - m0)
 
         nc.vector.memset(tab_s[:].bitcast(I32), 0)
-        nc.vector.memset(w4_raw_s[:].bitcast(I32), 0)
+        nc.gpsimd.memset(w4_raw_s[:].bitcast(I32), 0)
         nc.vector.memset(eps[:], 0.25)
         warm = keep.tile([P, 1], F32, name="warm")
         nc.scalar.activation(out=warm[:], in_=eps[:], func=ACT.Sqrt)
@@ -159,23 +175,27 @@ def tile_list_titanium_shock_pairs_kernel(
         load_w1(0, 0, W_AREA)
         nc.sync.dma_start(offs_sb[:], offs)
         load_tab(0)
-        nc.sync.dma_start(out=gain_sb[:], in_=gain.rearrange("(b p t) -> p b t", p=P, t=PACK))
         for q in range(QUADRANTS):
             nc.gpsimd.dma_start(
                 out=tab_s[QUADRANT * q + PACK : QUADRANT * q + PACK * (K_PASSES + 1), :].bitcast(I32),
                 in_=tab_scales[:, PACK * q : PACK * (q + 1), :].bitcast(I32),
             )
-        load_tab(1)
-        nc.sync.dma_start(pos1_sb[:], pos1)
-        nc.sync.dma_start(pos2_sb[:], pos2)
-        for q in range(QUADRANTS):
             nc.sync.dma_start(
                 out=w4_raw_s[QUADRANT * q : QUADRANT * q + PACK, :, :].bitcast(I32),
                 in_=w4_scales[:, PACK * q : PACK * (q + 1), :].rearrange("a r n -> r a n").bitcast(I32),
             )
+        nc.sync.dma_start(out=gain_sb[:], in_=gain.rearrange("(b p t) -> p b t", p=P, t=PACK))
+        load_tab(1)
+        nc.sync.dma_start(pos1_sb[:], pos1)
+        nc.sync.dma_start(pos2_sb[:], pos2)
+        load_w1(1, 0, W_AREA + W_BYTES)
+        load_tab(2)
+        load_w1(2, 0, W_AREA + 2 * W_BYTES)
+        w4_raw = keep.tile([P, BLOCKS, 2 * H], U8, name="w4_raw")
+        nc.sync.dma_start(out=w4_raw[:].bitcast(I32), in_=w4_words.rearrange("a p n -> p a n").bitcast(I32))
 
         cast_w1(0, 0, 0)
-        load_w1(1, 0, W_AREA + W_BYTES)
+        load_w1(0, 1, W_AREA)
         for b in range(BLOCKS):
             for t in range(PACK):
                 gain_row[b, t] = keep.tile([P, PAIRS], F32, name="gain_row%d%d" % (b, t))
@@ -183,68 +203,64 @@ def tile_list_titanium_shock_pairs_kernel(
         quantize_w1(0, 0, 1)
         for u in range(HALVES):
             gather_tab(0, u)
-        w4_raw = keep.tile([P, BLOCKS, 2 * H], U8, name="w4_raw")
-        nc.sync.dma_start(out=w4_raw[:].bitcast(I32), in_=w4_words.rearrange("a p n -> p a n").bitcast(I32))
-        load_tab(2)
-        for u in range(HALVES):
-            gather_tab(1, u)
-        v_s = areas.tile([P, S], U8, name="v_s", offset=TAB_BYTES, align_bytes=64)
+        v_s = areas.tile([P, S], U8, name="v_s", offset=0, align_bytes=64)
         nc.vector.tensor_copy(v_s[:], tab_s[:].indirect(offs_sb[:]))
-        for u in range(HALVES):
-            for t in range(PACK):
-                first_product(0, 0, t, u)
-        load_w1(2, 0, W_AREA + 2 * W_BYTES)
         nc.vector.tensor_copy(
             out=w4_s[:].rearrange("p a (c t m) -> p (a c) t m", t=PACK, m=P),
             in_=w4_raw_s[:].rearrange("p a (c m t) -> p (a c) t m", t=PACK, m=P),
         )
-        nc.vector.tensor_copy(
-            out=w4_c[:].bitcast(U16).rearrange("p a (c t m) -> p (a c) t m", t=PACK, m=P),
-            in_=w4_raw[:].bitcast(U16).rearrange("p a (c m t) -> p (a c) t m", t=PACK, m=P),
-        )
-        cast_w1(1, 0, 0)
-        load_w1(0, 1, W_AREA)
-        quantize_w1(1, 0, 1)
         for u in range(HALVES):
-            for t in range(PACK):
-                first_product(1, 0, t, u)
+            gather_tab(1, u)
+        load_w1(1, 1, TAB_BYTES)
+        load_w1(2, 1, TAB_BYTES + W_BYTES)
+        cast_w1(1, 0, 0)
+        quantize_w1(1, 0, 1)
+        for a in range(K_PASSES - 1):
+            for u in range(HALVES):
+                for t in range(PACK):
+                    first_product(a, 0, t, u)
         for u in range(HALVES):
             gather_tab(2, u)
-        load_w1(1, 1, 0)
-        load_w1(2, 1, W_BYTES)
         cast_w1_by_tiles(2, 0)
         quantize_w1(2, 0, 2)
         for t in range(PACK):
             for u in range(HALVES):
                 first_product(2, 0, t, u)
+        nc.vector.tensor_copy(
+            out=w4_c[:].bitcast(U16).rearrange("p a (c t m) -> p (a c) t m", t=PACK, m=P),
+            in_=w4_raw[:].bitcast(U16).rearrange("p a (c m t) -> p (a c) t m", t=PACK, m=P),
+        )
         for t in range(PACK):
             square_h(0, t)
 
         cast_w1(0, 1, P)
         pick_x(0, 0)
-        quantize_w1(0, 1, 1)
-        cast_w1(1, 1, MIDDLE_CAST_ON_VECTOR)
         pick_x(0, 1)
-        quantize_w1(1, 1, 1)
-        cast_w1(2, 1, LAST_CAST_ON_VECTOR)
+        quantize_w1(0, 1, 1)
+        cast_w1(1, 1, 0)
         pick_x(0, 2)
-        quantize_w1(2, 1, 1)
+        cast_w1(2, 1, LAST_CAST_ON_VECTOR)
+        quantize_late()
         pick_x(0, 3)
         for t in range(PACK):
             for u in range(HALVES):
                 first_product(0, 1, t, u)
         for t in range(PACK):
-            for a in range(1, K_PASSES):
-                for u in range(HALVES):
+            for u in range(HALVES):
+                for a in range(1, K_PASSES):
                     first_product(a, 1, t, u)
         for t in range(PACK):
             square_h(1, t)
-            pick_x(1, t)
+            if t < PACK - 1:
+                pick_x(1, t)
+        pick_x(1, PACK - 1, 0, MID)
+        pick_x(1, PACK - 1, MID, PAIRS)
         round_x(0, False)
         round_x(1, True)
-        quantize_x(1)
-        quantize_x(0)
-        first_pick = keep.tile([P, PAIRS], F32, name="first_pick", tag="x_bf0", align_bytes=64)
+        quantize_x(1, 0, MID)
+        quantize_x(0, 0, PAIRS)
+        quantize_x(1, MID, PAIRS)
+        first_pick = keep.tile([P, PAIRS], F32, name="first_pick", tag="x_bf1", align_bytes=64)
         nc.vector.tensor_copy(first_pick[:], h[0, 0][:].indirect(pos2_sb[:]))
 
         out_rows = out.rearrange("(b p t) m -> b t p m", p=P, t=PACK)
@@ -258,15 +274,15 @@ def tile_list_titanium_shock_pairs_kernel(
         def second_product(b, t):
             y = psum.tile([P, PAIRS], F32, name="bank")
             col = b * SPAN + t * P
-            for a in reversed(range(BLOCKS)):
+            for a in range(BLOCKS):
                 nc.tensor.matmul_mx(
                     out=y[:],
                     lhsT=w4_c[:, a, 2 * col : 2 * (col + P)].bitcast(FP4X4),
                     lhsT_scale=w4_s[:, a, col : col + P],
                     rhs=x_c[a][:].bitcast(FP8X4),
                     rhs_scale=x_s[a][:],
-                    start=(a == BLOCKS - 1),
-                    stop=(a == 0),
+                    start=(a == 0),
+                    stop=(a == BLOCKS - 1),
                 )
             y_sq[b, t] = stage.tile([P, PAIRS], F32, name="y_sq", bufs=SQRT_LAG + 2)
             nc.scalar.activation(out=y_sq[b, t][:], in_=y[:], func=ACT.Square)
@@ -287,7 +303,8 @@ def tile_list_titanium_shock_pairs_kernel(
             for m0, m1 in pieces(b, t):
                 part = total[b, t][:, m0:m1]
                 nc.scalar.activation(out=part, in_=part, func=ACT.Sqrt, bias=eps[:])
-                nc.sync.dma_start(out=out_rows[b, t][:, m0:m1], in_=part)
+                queue = nc.scalar if ((b, t), m1) == (row_tiles[-1], PAIRS) else nc.sync
+                queue.dma_start(out=out_rows[b, t][:, m0:m1], in_=part)
 
         for i in range(len(row_tiles) + SQRT_LAG):
             if i < len(row_tiles):

@@ -27,6 +27,7 @@ QUADRANTS = P // QUADRANT
 PER_COLUMN = 16
 MID = PAIRS // 2
 RUN = 4
+EARLY_TILES = 2
 SQRT_LAG = 2
 
 LAST_CAST_ON_VECTOR = 80
@@ -63,7 +64,8 @@ def tile_list_titanium_shock_pairs_kernel(
             x_f1[:].rearrange("p (t m) -> p t m", t=PACK),
         ]
         tab_w, gain_row, v_c, w_raw, w_bf, w_c, w_s = {}, {}, {}, {}, {}, {}, {}
-        h_sum, h, x_bf, x_c, x_s, y_sq, total = {}, {}, {}, {}, {}, {}, {}
+        h_sum, h, x_bf, x_c, x_s, total = {}, {}, {}, {}, {}, {}
+        halves = [(0, MID), (MID, PAIRS)]
 
         def load_w1(a, b, offset):
             w_raw[a, b] = areas.tile([P, PACK, SPAN], F32, name="w_raw%d%d" % (a, b), offset=offset)
@@ -150,15 +152,15 @@ def tile_list_titanium_shock_pairs_kernel(
                 x_f[b][:, t, m0:m1], h[b, t][:].indirect(entries), gain_row[b, t][:, m0:m1], ALU.mult
             )
 
-        def round_x(b, on_vector):
-            x_bf[b] = keep.tile([P, PAIRS * PACK], BF16, name="x_bf", tag="x_bf%d" % b, align_bytes=64)
-            dst = x_bf[b][:].rearrange("p (c i t) -> p c t i", i=RUN, t=PACK)
-            src = x_f[b].rearrange("p t (c i) -> p c t i", i=RUN)
-            if on_vector:
-                nc.vector.tensor_copy(out=dst[:, : MID // RUN], in_=src[:, : MID // RUN])
-                nc.vector.tensor_copy(out=dst[:, MID // RUN :], in_=src[:, MID // RUN :])
-            else:
+        def round_x(b, m0, m1):
+            if m0 == 0:
+                x_bf[b] = keep.tile([P, PAIRS * PACK], BF16, name="x_bf", tag="x_bf%d" % b, align_bytes=64)
+            dst = x_bf[b][:, PACK * m0 : PACK * m1].rearrange("p (c i t) -> p c t i", i=RUN, t=PACK)
+            src = x_f[b][:, :, m0:m1].rearrange("p t (c i) -> p c t i", i=RUN)
+            if b == 0:
                 nc.scalar.copy(out=dst, in_=src)
+            else:
+                nc.vector.tensor_copy(out=dst, in_=src)
 
         def quantize_x(b, m0, m1):
             if m0 == 0:
@@ -235,9 +237,9 @@ def tile_list_titanium_shock_pairs_kernel(
 
         cast_w1(0, 1, P)
         pick_x(0, 0)
-        pick_x(0, 1)
         quantize_w1(0, 1, 1)
         cast_w1(1, 1, 0)
+        pick_x(0, 1)
         pick_x(0, 2)
         cast_w1(2, 1, LAST_CAST_ON_VECTOR)
         quantize_late()
@@ -253,61 +255,59 @@ def tile_list_titanium_shock_pairs_kernel(
             square_h(1, t)
             if t < PACK - 1:
                 pick_x(1, t)
-        pick_x(1, PACK - 1, 0, MID)
-        pick_x(1, PACK - 1, MID, PAIRS)
-        round_x(0, False)
-        round_x(1, True)
-        quantize_x(1, 0, MID)
-        quantize_x(0, 0, PAIRS)
-        quantize_x(1, MID, PAIRS)
-        first_pick = keep.tile([P, PAIRS], F32, name="first_pick", tag="x_bf1", align_bytes=64)
-        nc.vector.tensor_copy(first_pick[:], h[0, 0][:].indirect(pos2_sb[:]))
+        for m0, m1 in halves:
+            pick_x(1, PACK - 1, m0, m1)
+        for m0, m1 in halves:
+            for b in range(BLOCKS):
+                round_x(b, m0, m1)
+            for b in range(BLOCKS):
+                quantize_x(b, m0, m1)
 
         out_rows = out.rearrange("(b p t) m -> b t p m", p=P, t=PACK)
         row_tiles = [(b, t) for b in range(BLOCKS) for t in range(PACK)]
 
-        def pieces(b, t):
-            if (b, t) == row_tiles[-1]:
-                return [(0, MID), (MID, PAIRS)]
-            return [(0, PAIRS)]
-
-        def second_product(b, t):
-            y = psum.tile([P, PAIRS], F32, name="bank")
+        def second_product(b, t, m0, m1):
+            y = psum.tile([P, m1 - m0], F32, name="bank")
             col = b * SPAN + t * P
-            for a in range(BLOCKS):
-                nc.tensor.matmul_mx(
-                    out=y[:],
-                    lhsT=w4_c[:, a, 2 * col : 2 * (col + P)].bitcast(FP4X4),
-                    lhsT_scale=w4_s[:, a, col : col + P],
-                    rhs=x_c[a][:].bitcast(FP8X4),
-                    rhs_scale=x_s[a][:],
-                    start=(a == 0),
-                    stop=(a == BLOCKS - 1),
-                )
-            y_sq[b, t] = stage.tile([P, PAIRS], F32, name="y_sq", bufs=SQRT_LAG + 2)
-            nc.scalar.activation(out=y_sq[b, t][:], in_=y[:], func=ACT.Square)
-            offset = 2 * TAB_BYTES + 4 * PAIRS * (PACK * b + t)
-            total[b, t] = areas.tile([P, PAIRS], F32, name="total%d%d" % (b, t), offset=offset)
-            if (b, t) == row_tiles[0]:
-                nc.vector.tensor_tensor(total[b, t][:], first_pick[:], y_sq[b, t][:], ALU.add)
-            else:
-                for m0, m1 in pieces(b, t):
-                    nc.vector.tensor_tensor(
-                        total[b, t][:, m0:m1],
-                        h[b, t][:].indirect(pos2_sb[:, m0 // PER_COLUMN : m1 // PER_COLUMN]),
-                        y_sq[b, t][:, m0:m1],
-                        ALU.add,
+            width = PAIRS if m1 - m0 == PAIRS else P
+            for m in range(m0, m1, width):
+                for a in range(BLOCKS):
+                    nc.tensor.matmul_mx(
+                        out=y[:, m - m0 : m - m0 + width],
+                        lhsT=w4_c[:, a, 2 * col : 2 * (col + P)].bitcast(FP4X4),
+                        lhsT_scale=w4_s[:, a, col : col + P],
+                        rhs=x_c[a][:, m : m + width].bitcast(FP8X4),
+                        rhs_scale=x_s[a][:, m : m + width],
+                        start=(a == 0),
+                        stop=(a == BLOCKS - 1),
                     )
+            y_sq = stage.tile([P, m1 - m0], F32, name="y_sq", bufs=SQRT_LAG + 2)
+            nc.scalar.activation(out=y_sq[:], in_=y[:], func=ACT.Square)
+            if m0 == 0:
+                offset = 2 * TAB_BYTES + 4 * PAIRS * (PACK * b + t)
+                total[b, t] = areas.tile([P, PAIRS], F32, name="total%d%d" % (b, t), offset=offset)
+            for n0, n1 in pieces(b, t, m0, m1):
+                nc.vector.tensor_tensor(
+                    total[b, t][:, n0:n1],
+                    h[b, t][:].indirect(pos2_sb[:, n0 // PER_COLUMN : n1 // PER_COLUMN]),
+                    y_sq[:, n0 - m0 : n1 - m0],
+                    ALU.add,
+                )
+
+        def pieces(b, t, m0, m1):
+            return halves if (b, t) == row_tiles[-1] else [(m0, m1)]
 
         def finish(b, t):
-            for m0, m1 in pieces(b, t):
+            for m0, m1 in pieces(b, t, 0, PAIRS):
                 part = total[b, t][:, m0:m1]
                 nc.scalar.activation(out=part, in_=part, func=ACT.Sqrt, bias=eps[:])
                 queue = nc.scalar if ((b, t), m1) == (row_tiles[-1], PAIRS) else nc.sync
                 queue.dma_start(out=out_rows[b, t][:, m0:m1], in_=part)
 
-        for i in range(len(row_tiles) + SQRT_LAG):
+        for m0, m1 in halves:
+            for b, t in row_tiles[:EARLY_TILES]:
+                second_product(b, t, m0, m1)
+        for i in range(EARLY_TILES, len(row_tiles) + SQRT_LAG):
             if i < len(row_tiles):
-                second_product(*row_tiles[i])
-            if i >= SQRT_LAG:
-                finish(*row_tiles[i - SQRT_LAG])
+                second_product(*row_tiles[i], 0, PAIRS)
+            finish(*row_tiles[i - SQRT_LAG])

@@ -27,6 +27,10 @@ QUADRANTS = P // QUADRANT
 PER_COLUMN = 16
 MID = PAIRS // 2
 RUN = 4
+ALL_TILES = [(0, PACK)]
+TILE_PAIRS = [(0, 2), (2, PACK)]
+FIRST_TILES_FIRST = [(0, 1), (1, 2), (2, PACK)]
+LAST_PIECE = 128
 EARLY_TILES = 2
 SQRT_LAG = 2
 
@@ -97,18 +101,15 @@ def tile_list_titanium_shock_pairs_kernel(
             nc.vector.tensor_copy(out=dst[:, :, :, :2], in_=src[:, :, :, :2])
             nc.scalar.copy(out=dst[:, :, :, 2:], in_=src[:, :, :, 2:])
 
-        def quantize(codes, scales, values, width):
-            for c in range(0, codes.shape[1], width):
-                nc.vector.quantize_mx(
-                    out=codes[:, c : c + width].bitcast(FP8X4),
-                    scales=scales[:, c : c + width],
-                    in_=values[:, PACK * c : PACK * (c + width)],
-                )
+        def quantize(codes, scales, values):
+            nc.vector.quantize_mx(out=codes.bitcast(FP8X4), scales=scales, in_=values)
 
-        def quantize_w1(a, b, parts):
+        def quantize_w1(a, b, tile_runs):
             codes = keep.tile([P, SPAN], U32, name="w_c%d%d" % (a, b), align_bytes=64)
             scales = keep.tile([P, SPAN], U8, name="w_s%d%d" % (a, b), align_bytes=64)
-            quantize(codes, scales, w_bf[a, b], SPAN // parts)
+            for t0, t1 in tile_runs:
+                cols = slice(t0 * P, t1 * P)
+                quantize(codes[:, cols], scales[:, cols], w_bf[a, b][:, t0 * SPAN : t1 * SPAN])
             for t in range(PACK):
                 w_c[a, b, t] = codes[:, t * P : (t + 1) * P]
                 w_s[a, b, t] = scales[:, t * P : (t + 1) * P]
@@ -116,7 +117,9 @@ def tile_list_titanium_shock_pairs_kernel(
         def quantize_late():
             codes = keep.tile([P, 2 * SPAN], U32, name="late_c", tag="x_bf0", align_bytes=64)
             scales = keep.tile([P, 2 * SPAN], U8, name="late_s", align_bytes=64)
-            quantize(codes, scales, late_bf, SPAN)
+            for t0, t1 in FIRST_TILES_FIRST:
+                cols = slice(2 * t0 * P, 2 * t1 * P)
+                quantize(codes[:, cols], scales[:, cols], late_bf[:, 2 * t0 * SPAN : 2 * t1 * SPAN])
             for t in range(PACK):
                 for a in (1, 2):
                     cols = slice((2 * t + a - 1) * P, (2 * t + a) * P)
@@ -153,9 +156,7 @@ def tile_list_titanium_shock_pairs_kernel(
             )
 
         def round_x(b, m0, m1):
-            if m0 == 0:
-                x_bf[b] = keep.tile([P, PAIRS * PACK], BF16, name="x_bf", tag="x_bf%d" % b, align_bytes=64)
-            dst = x_bf[b][:, PACK * m0 : PACK * m1].rearrange("p (c i t) -> p c t i", i=RUN, t=PACK)
+            dst = x_bf[b, m0].rearrange("p (c i t) -> p c t i", i=RUN, t=PACK)
             src = x_f[b][:, :, m0:m1].rearrange("p t (c i) -> p c t i", i=RUN)
             if b == 0:
                 nc.scalar.copy(out=dst, in_=src)
@@ -166,7 +167,7 @@ def tile_list_titanium_shock_pairs_kernel(
             if m0 == 0:
                 x_c[b] = keep.tile([P, PAIRS], U32, name="x_c%d" % b, align_bytes=64)
                 x_s[b] = keep.tile([P, PAIRS], U8, name="x_s%d" % b, align_bytes=64)
-            quantize(x_c[b][:, m0:m1], x_s[b][:, m0:m1], x_bf[b][:, PACK * m0 : PACK * m1], m1 - m0)
+            quantize(x_c[b][:, m0:m1], x_s[b][:, m0:m1], x_bf[b, m0])
 
         nc.vector.memset(tab_s[:].bitcast(I32), 0)
         nc.gpsimd.memset(w4_raw_s[:].bitcast(I32), 0)
@@ -202,7 +203,7 @@ def tile_list_titanium_shock_pairs_kernel(
             for t in range(PACK):
                 gain_row[b, t] = keep.tile([P, PAIRS], F32, name="gain_row%d%d" % (b, t))
                 nc.scalar.copy(out=gain_row[b, t][:], in_=gain_sb[:, b, t : t + 1].to_broadcast([P, PAIRS]))
-        quantize_w1(0, 0, 1)
+        quantize_w1(0, 0, ALL_TILES)
         for u in range(HALVES):
             gather_tab(0, u)
         v_s = areas.tile([P, S], U8, name="v_s", offset=0, align_bytes=64)
@@ -216,7 +217,7 @@ def tile_list_titanium_shock_pairs_kernel(
         load_w1(1, 1, TAB_BYTES)
         load_w1(2, 1, TAB_BYTES + W_BYTES)
         cast_w1(1, 0, 0)
-        quantize_w1(1, 0, 1)
+        quantize_w1(1, 0, ALL_TILES)
         for a in range(K_PASSES - 1):
             for u in range(HALVES):
                 for t in range(PACK):
@@ -224,7 +225,7 @@ def tile_list_titanium_shock_pairs_kernel(
         for u in range(HALVES):
             gather_tab(2, u)
         cast_w1_by_tiles(2, 0)
-        quantize_w1(2, 0, 2)
+        quantize_w1(2, 0, TILE_PAIRS)
         for t in range(PACK):
             for u in range(HALVES):
                 first_product(2, 0, t, u)
@@ -237,7 +238,7 @@ def tile_list_titanium_shock_pairs_kernel(
 
         cast_w1(0, 1, P)
         pick_x(0, 0)
-        quantize_w1(0, 1, 1)
+        quantize_w1(0, 1, ALL_TILES)
         cast_w1(1, 1, 0)
         pick_x(0, 1)
         pick_x(0, 2)
@@ -255,6 +256,10 @@ def tile_list_titanium_shock_pairs_kernel(
             square_h(1, t)
             if t < PACK - 1:
                 pick_x(1, t)
+        x_bf0 = keep.tile([P, PAIRS * PACK], BF16, name="x_bf0", tag="x_bf0", align_bytes=64)
+        x_bf1 = keep.tile([P, MID * PACK], BF16, name="x_bf1", align_bytes=64)
+        x_bf[0, 0], x_bf[0, MID] = x_bf0[:, : MID * PACK], x_bf0[:, MID * PACK :]
+        x_bf[1, 0], x_bf[1, MID] = x_bf1[:], x_bf[0, 0]
         for m0, m1 in halves:
             pick_x(1, PACK - 1, m0, m1)
         for m0, m1 in halves:
@@ -295,7 +300,9 @@ def tile_list_titanium_shock_pairs_kernel(
                 )
 
         def pieces(b, t, m0, m1):
-            return halves if (b, t) == row_tiles[-1] else [(m0, m1)]
+            if (b, t) == row_tiles[-1]:
+                return [(0, MID), (MID, PAIRS - LAST_PIECE), (PAIRS - LAST_PIECE, PAIRS)]
+            return [(m0, m1)]
 
         def finish(b, t):
             for m0, m1 in pieces(b, t, 0, PAIRS):

@@ -30,7 +30,6 @@ RUN = 4
 ALL_TILES = [(0, PACK)]
 TILE_PAIRS = [(0, 2), (2, PACK)]
 FIRST_TILES_FIRST = [(0, 1), (1, 2), (2, PACK)]
-LAST_PIECE = 128
 EARLY_TILES = 2
 SQRT_LAG = 2
 
@@ -156,12 +155,12 @@ def tile_list_titanium_shock_pairs_kernel(
             )
 
         def round_x(b, m0, m1):
-            dst = x_bf[b, m0].rearrange("p (c i t) -> p c t i", i=RUN, t=PACK)
-            src = x_f[b][:, :, m0:m1].rearrange("p t (c i) -> p c t i", i=RUN)
             if b == 0:
-                nc.scalar.copy(out=dst, in_=src)
+                dst = x_bf[b, m0].rearrange("p (m t) -> p m t", t=PACK)
+                nc.scalar.copy(out=dst, in_=x_f[b][:, :, m0:m1].rearrange("p t m -> p m t"))
             else:
-                nc.vector.tensor_copy(out=dst, in_=src)
+                dst = x_bf[b, m0].rearrange("p (c i t) -> p c t i", i=RUN, t=PACK)
+                nc.vector.tensor_copy(out=dst, in_=x_f[b][:, :, m0:m1].rearrange("p t (c i) -> p c t i", i=RUN))
 
         def quantize_x(b, m0, m1):
             if m0 == 0:
@@ -300,9 +299,7 @@ def tile_list_titanium_shock_pairs_kernel(
                 )
 
         def pieces(b, t, m0, m1):
-            if (b, t) == row_tiles[-1]:
-                return [(0, MID), (MID, PAIRS - LAST_PIECE), (PAIRS - LAST_PIECE, PAIRS)]
-            return [(m0, m1)]
+            return halves if (b, t) == row_tiles[-1] else [(m0, m1)]
 
         def finish(b, t):
             for m0, m1 in pieces(b, t, 0, PAIRS):

@@ -83,7 +83,10 @@ def tile_list_titanium_shock_pairs_kernel(
             if a > 0 and b == 1:
                 dst = late_bf.rearrange("p (t a m j) -> p a m j t", t=PACK, a=2, j=PACK)[:, a - 1]
             else:
-                w_bf[a, b] = stage.tile([P, PACK * SPAN], BF16, name="w_bf", align_bytes=64)[:]
+                if b == 1:
+                    w_bf[a, b] = x_f0[:, PAIRS : 3 * PAIRS].bitcast(BF16)
+                else:
+                    w_bf[a, b] = stage.tile([P, PACK * SPAN], BF16, name="w_bf", align_bytes=64)[:]
                 dst = w_bf[a, b].rearrange("p (t m j) -> p m j t", t=PACK, j=PACK)
             src = w_raw[a, b][:].rearrange("p j (m t) -> p m j t", t=PACK)
             return dst, src
@@ -200,8 +203,11 @@ def tile_list_titanium_shock_pairs_kernel(
         load_w1(0, 1, W_AREA)
         for b in range(BLOCKS):
             for t in range(PACK):
-                gain_row[b, t] = keep.tile([P, PAIRS], F32, name="gain_row%d%d" % (b, t))
-                nc.scalar.copy(out=gain_row[b, t][:], in_=gain_sb[:, b, t : t + 1].to_broadcast([P, PAIRS]))
+                if (b, t) == (0, 0):
+                    gain_row[b, t] = x_f0[:, PAIRS : 2 * PAIRS]
+                else:
+                    gain_row[b, t] = keep.tile([P, PAIRS], F32, name="gain_row%d%d" % (b, t))[:]
+                nc.scalar.copy(out=gain_row[b, t], in_=gain_sb[:, b, t : t + 1].to_broadcast([P, PAIRS]))
         quantize_w1(0, 0, ALL_TILES)
         for u in range(HALVES):
             gather_tab(0, u)
@@ -235,9 +241,11 @@ def tile_list_titanium_shock_pairs_kernel(
         for t in range(PACK):
             square_h(0, t)
 
-        cast_w1(0, 1, P)
         pick_x(0, 0)
-        quantize_w1(0, 1, ALL_TILES)
+        dst, src = cast_views(0, 1)
+        for t0, t1 in TILE_PAIRS:
+            nc.vector.tensor_copy(out=dst[:, :, :, t0:t1], in_=src[:, :, :, t0:t1])
+        quantize_w1(0, 1, TILE_PAIRS)
         cast_w1(1, 1, 0)
         pick_x(0, 1)
         pick_x(0, 2)

@@ -33,11 +33,12 @@ FIRST_TILES_FIRST = [(0, 1), (1, 2), (2, PACK)]
 EARLY_TILES = 2
 SQRT_LAG = 2
 
-LAST_CAST_ON_VECTOR = 80
+LAST_CAST_ON_VECTOR = (84, 40)
 
 TAB_BYTES = 4 * T
 W_BYTES = 4 * PACK * SPAN
-W_AREA = K_PASSES * TAB_BYTES
+TAB_AREA = BLOCKS * H
+W_AREA = TAB_AREA + K_PASSES * TAB_BYTES
 
 
 def tile_list_titanium_shock_pairs_kernel(
@@ -54,7 +55,7 @@ def tile_list_titanium_shock_pairs_kernel(
         pos1_sb = keep.tile([P, PAIRS // PER_COLUMN], U16, name="pos1_sb")
         pos2_sb = keep.tile([P, PAIRS // PER_COLUMN], U16, name="pos2_sb")
         tab_s = keep.tile([P, T], U8, name="tab_s")
-        w4_raw_s = keep.tile([P, BLOCKS, H], U8, name="w4_raw_s")
+        w4_raw_s = areas.tile([P, BLOCKS, H], U8, name="w4_raw_s", offset=0)
         w4_c = keep.tile([P, BLOCKS, 2 * H], U8, name="w4_c", align_bytes=64)
         w4_s = keep.tile([P, BLOCKS, H], U8, name="w4_s", align_bytes=64)
         gain_sb = keep.tile([P, BLOCKS, PACK], F32, name="gain_sb")
@@ -76,7 +77,7 @@ def tile_list_titanium_shock_pairs_kernel(
             nc.sync.dma_start(out=w_raw[a, b][:], in_=rows.rearrange("(p j) c -> p j c", j=PACK))
 
         def load_tab(a):
-            tab_w[a] = areas.tile([P, T], I32, name="tab_w%d" % a, offset=a * TAB_BYTES)
+            tab_w[a] = areas.tile([P, T], I32, name="tab_w%d" % a, offset=TAB_AREA + a * TAB_BYTES)
             nc.sync.dma_start(out=tab_w[a][:], in_=tab_words[a].rearrange("p t i -> p (t i)").bitcast(I32))
 
         def cast_views(a, b):
@@ -102,6 +103,12 @@ def tile_list_titanium_shock_pairs_kernel(
             dst, src = cast_views(a, b)
             nc.vector.tensor_copy(out=dst[:, :, :, :2], in_=src[:, :, :, :2])
             nc.scalar.copy(out=dst[:, :, :, 2:], in_=src[:, :, :, 2:])
+
+        def cast_w1_by_pairs(a, b, shares):
+            dst, src = cast_views(a, b)
+            for (t0, t1), on_vector in zip(TILE_PAIRS, shares):
+                nc.vector.tensor_copy(out=dst[:, :on_vector, :, t0:t1], in_=src[:, :on_vector, :, t0:t1])
+                nc.scalar.copy(out=dst[:, on_vector:, :, t0:t1], in_=src[:, on_vector:, :, t0:t1])
 
         def quantize(codes, scales, values):
             nc.vector.quantize_mx(out=codes.bitcast(FP8X4), scales=scales, in_=values)
@@ -178,8 +185,8 @@ def tile_list_titanium_shock_pairs_kernel(
         nc.scalar.activation(out=warm[:], in_=eps[:], func=ACT.Sqrt)
 
         load_w1(0, 0, W_AREA)
-        nc.sync.dma_start(offs_sb[:], offs)
         load_tab(0)
+        nc.sync.dma_start(offs_sb[:], offs)
         for q in range(QUADRANTS):
             nc.gpsimd.dma_start(
                 out=tab_s[QUADRANT * q + PACK : QUADRANT * q + PACK * (K_PASSES + 1), :].bitcast(I32),
@@ -191,11 +198,11 @@ def tile_list_titanium_shock_pairs_kernel(
             )
         nc.sync.dma_start(out=gain_sb[:], in_=gain.rearrange("(b p t) -> p b t", p=P, t=PACK))
         load_tab(1)
-        nc.sync.dma_start(pos1_sb[:], pos1)
-        nc.sync.dma_start(pos2_sb[:], pos2)
         load_w1(1, 0, W_AREA + W_BYTES)
         load_tab(2)
         load_w1(2, 0, W_AREA + 2 * W_BYTES)
+        nc.sync.dma_start(pos1_sb[:], pos1)
+        nc.sync.dma_start(pos2_sb[:], pos2)
         w4_raw = keep.tile([P, BLOCKS, 2 * H], U8, name="w4_raw")
         nc.sync.dma_start(out=w4_raw[:].bitcast(I32), in_=w4_words.rearrange("a p n -> p a n").bitcast(I32))
 
@@ -211,16 +218,16 @@ def tile_list_titanium_shock_pairs_kernel(
         quantize_w1(0, 0, ALL_TILES)
         for u in range(HALVES):
             gather_tab(0, u)
-        v_s = areas.tile([P, S], U8, name="v_s", offset=0, align_bytes=64)
-        nc.vector.tensor_copy(v_s[:], tab_s[:].indirect(offs_sb[:]))
         nc.vector.tensor_copy(
             out=w4_s[:].rearrange("p a (c t m) -> p (a c) t m", t=PACK, m=P),
             in_=w4_raw_s[:].rearrange("p a (c m t) -> p (a c) t m", t=PACK, m=P),
         )
+        v_s = areas.tile([P, S], U8, name="v_s", offset=TAB_AREA - S // 2, align_bytes=64)
+        nc.vector.tensor_copy(v_s[:], tab_s[:].indirect(offs_sb[:]))
         for u in range(HALVES):
             gather_tab(1, u)
-        load_w1(1, 1, TAB_BYTES)
-        load_w1(2, 1, TAB_BYTES + W_BYTES)
+        load_w1(1, 1, TAB_AREA + TAB_BYTES)
+        load_w1(2, 1, TAB_AREA + TAB_BYTES + W_BYTES)
         cast_w1(1, 0, 0)
         quantize_w1(1, 0, ALL_TILES)
         for a in range(K_PASSES - 1):
@@ -249,7 +256,7 @@ def tile_list_titanium_shock_pairs_kernel(
         cast_w1(1, 1, 0)
         pick_x(0, 1)
         pick_x(0, 2)
-        cast_w1(2, 1, LAST_CAST_ON_VECTOR)
+        cast_w1_by_pairs(2, 1, LAST_CAST_ON_VECTOR)
         quantize_late()
         pick_x(0, 3)
         for t in range(PACK):
@@ -296,7 +303,7 @@ def tile_list_titanium_shock_pairs_kernel(
             y_sq = stage.tile([P, m1 - m0], F32, name="y_sq", bufs=SQRT_LAG + 2)
             nc.scalar.activation(out=y_sq[:], in_=y[:], func=ACT.Square)
             if m0 == 0:
-                offset = 2 * TAB_BYTES + 4 * PAIRS * (PACK * b + t)
+                offset = TAB_AREA + 2 * TAB_BYTES + 4 * PAIRS * (PACK * b + t)
                 total[b, t] = areas.tile([P, PAIRS], F32, name="total%d%d" % (b, t), offset=offset)
             for n0, n1 in pieces(b, t, m0, m1):
                 nc.vector.tensor_tensor(

@@ -33,12 +33,12 @@ FIRST_TILES_FIRST = [(0, 1), (1, 2), (2, PACK)]
 EARLY_TILES = 2
 SQRT_LAG = 2
 
+PAIR_CAST_ON_VECTOR = (56, 40)
 LAST_CAST_ON_VECTOR = (84, 40)
 
 TAB_BYTES = 4 * T
 W_BYTES = 4 * PACK * SPAN
-TAB_AREA = BLOCKS * H
-W_AREA = TAB_AREA + K_PASSES * TAB_BYTES
+W_AREA = K_PASSES * TAB_BYTES
 
 
 def tile_list_titanium_shock_pairs_kernel(
@@ -55,7 +55,7 @@ def tile_list_titanium_shock_pairs_kernel(
         pos1_sb = keep.tile([P, PAIRS // PER_COLUMN], U16, name="pos1_sb")
         pos2_sb = keep.tile([P, PAIRS // PER_COLUMN], U16, name="pos2_sb")
         tab_s = keep.tile([P, T], U8, name="tab_s")
-        w4_raw_s = areas.tile([P, BLOCKS, H], U8, name="w4_raw_s", offset=0)
+        w4_raw_s = keep.tile([P, BLOCKS, H], U8, name="w4_raw_s")
         w4_c = keep.tile([P, BLOCKS, 2 * H], U8, name="w4_c", align_bytes=64)
         w4_s = keep.tile([P, BLOCKS, H], U8, name="w4_s", align_bytes=64)
         gain_sb = keep.tile([P, BLOCKS, PACK], F32, name="gain_sb")
@@ -77,7 +77,7 @@ def tile_list_titanium_shock_pairs_kernel(
             nc.sync.dma_start(out=w_raw[a, b][:], in_=rows.rearrange("(p j) c -> p j c", j=PACK))
 
         def load_tab(a):
-            tab_w[a] = areas.tile([P, T], I32, name="tab_w%d" % a, offset=TAB_AREA + a * TAB_BYTES)
+            tab_w[a] = areas.tile([P, T], I32, name="tab_w%d" % a, offset=a * TAB_BYTES)
             nc.sync.dma_start(out=tab_w[a][:], in_=tab_words[a].rearrange("p t i -> p (t i)").bitcast(I32))
 
         def cast_views(a, b):
@@ -98,11 +98,6 @@ def tile_list_titanium_shock_pairs_kernel(
                 nc.vector.tensor_copy(out=dst[:, :on_vector], in_=src[:, :on_vector])
             if on_vector < P:
                 nc.scalar.copy(out=dst[:, on_vector:], in_=src[:, on_vector:])
-
-        def cast_w1_by_tiles(a, b):
-            dst, src = cast_views(a, b)
-            nc.vector.tensor_copy(out=dst[:, :, :, :2], in_=src[:, :, :, :2])
-            nc.scalar.copy(out=dst[:, :, :, 2:], in_=src[:, :, :, 2:])
 
         def cast_w1_by_pairs(a, b, shares):
             dst, src = cast_views(a, b)
@@ -222,12 +217,14 @@ def tile_list_titanium_shock_pairs_kernel(
             out=w4_s[:].rearrange("p a (c t m) -> p (a c) t m", t=PACK, m=P),
             in_=w4_raw_s[:].rearrange("p a (c m t) -> p (a c) t m", t=PACK, m=P),
         )
-        v_s = areas.tile([P, S], U8, name="v_s", offset=TAB_AREA - S // 2, align_bytes=64)
-        nc.vector.tensor_copy(v_s[:], tab_s[:].indirect(offs_sb[:]))
         for u in range(HALVES):
             gather_tab(1, u)
-        load_w1(1, 1, TAB_AREA + TAB_BYTES)
-        load_w1(2, 1, TAB_AREA + TAB_BYTES + W_BYTES)
+        v_s = areas.tile([P, S], U8, name="v_s", offset=TAB_BYTES, align_bytes=64)
+        for u in range(HALVES):
+            entries = offs_sb[:, u * SPAN // PER_COLUMN : (u + 1) * SPAN // PER_COLUMN]
+            nc.vector.tensor_copy(v_s[:, u * SPAN : (u + 1) * SPAN], tab_s[:].indirect(entries))
+        load_w1(1, 1, 0)
+        load_w1(2, 1, W_BYTES)
         cast_w1(1, 0, 0)
         quantize_w1(1, 0, ALL_TILES)
         for a in range(K_PASSES - 1):
@@ -236,7 +233,7 @@ def tile_list_titanium_shock_pairs_kernel(
                     first_product(a, 0, t, u)
         for u in range(HALVES):
             gather_tab(2, u)
-        cast_w1_by_tiles(2, 0)
+        cast_w1_by_pairs(2, 0, PAIR_CAST_ON_VECTOR)
         quantize_w1(2, 0, TILE_PAIRS)
         for t in range(PACK):
             for u in range(HALVES):
@@ -303,7 +300,7 @@ def tile_list_titanium_shock_pairs_kernel(
             y_sq = stage.tile([P, m1 - m0], F32, name="y_sq", bufs=SQRT_LAG + 2)
             nc.scalar.activation(out=y_sq[:], in_=y[:], func=ACT.Square)
             if m0 == 0:
-                offset = TAB_AREA + 2 * TAB_BYTES + 4 * PAIRS * (PACK * b + t)
+                offset = 2 * TAB_BYTES + 4 * PAIRS * (PACK * b + t)
                 total[b, t] = areas.tile([P, PAIRS], F32, name="total%d%d" % (b, t), offset=offset)
             for n0, n1 in pieces(b, t, m0, m1):
                 nc.vector.tensor_tensor(

@@ -71,13 +71,13 @@ def tile_list_titanium_shock_pairs_kernel(
         h_sum, h, x_bf, x_c, x_s, total = {}, {}, {}, {}, {}, {}
         halves = [(0, MID), (MID, PAIRS)]
 
-        def load_w1(a, b, offset):
+        def load_w1(a, b, offset, queue=nc.sync):
             w_raw[a, b] = areas.tile([P, PACK, SPAN], F32, name="w_raw%d%d" % (a, b), offset=offset)
             rows = w1[a * SPAN : (a + 1) * SPAN, b * SPAN : (b + 1) * SPAN]
-            nc.sync.dma_start(out=w_raw[a, b][:], in_=rows.rearrange("(p j) c -> p j c", j=PACK))
+            queue.dma_start(out=w_raw[a, b][:], in_=rows.rearrange("(p j) c -> p j c", j=PACK))
 
         def load_tab(a):
-            tab_w[a] = areas.tile([P, T], I32, name="tab_w%d" % a, offset=a * TAB_BYTES)
+            tab_w[a] = areas.tile([P, T], I32, name="tab_w%d" % a, offset=(1, 0, 2)[a] * TAB_BYTES)
             nc.sync.dma_start(out=tab_w[a][:], in_=tab_words[a].rearrange("p t i -> p (t i)").bitcast(I32))
 
         def cast_views(a, b):
@@ -173,13 +173,14 @@ def tile_list_titanium_shock_pairs_kernel(
                 x_s[b] = keep.tile([P, PAIRS], U8, name="x_s%d" % b, align_bytes=64)
             quantize(x_c[b][:, m0:m1], x_s[b][:, m0:m1], x_bf[b, m0])
 
+        load_w1(0, 0, W_AREA, nc.scalar)
+        load_w1(1, 0, W_AREA + W_BYTES, nc.scalar)
         nc.vector.memset(tab_s[:].bitcast(I32), 0)
         nc.gpsimd.memset(w4_raw_s[:].bitcast(I32), 0)
         nc.vector.memset(eps[:], 0.25)
         warm = keep.tile([P, 1], F32, name="warm")
         nc.scalar.activation(out=warm[:], in_=eps[:], func=ACT.Sqrt)
 
-        load_w1(0, 0, W_AREA)
         load_tab(0)
         nc.sync.dma_start(offs_sb[:], offs)
         for q in range(QUADRANTS):
@@ -193,7 +194,6 @@ def tile_list_titanium_shock_pairs_kernel(
             )
         nc.sync.dma_start(out=gain_sb[:], in_=gain.rearrange("(b p t) -> p b t", p=P, t=PACK))
         load_tab(1)
-        load_w1(1, 0, W_AREA + W_BYTES)
         load_tab(2)
         load_w1(2, 0, W_AREA + 2 * W_BYTES)
         nc.sync.dma_start(pos1_sb[:], pos1)
@@ -217,12 +217,12 @@ def tile_list_titanium_shock_pairs_kernel(
             out=w4_s[:].rearrange("p a (c t m) -> p (a c) t m", t=PACK, m=P),
             in_=w4_raw_s[:].rearrange("p a (c m t) -> p (a c) t m", t=PACK, m=P),
         )
-        for u in range(HALVES):
-            gather_tab(1, u)
         v_s = areas.tile([P, S], U8, name="v_s", offset=TAB_BYTES, align_bytes=64)
         for u in range(HALVES):
             entries = offs_sb[:, u * SPAN // PER_COLUMN : (u + 1) * SPAN // PER_COLUMN]
             nc.vector.tensor_copy(v_s[:, u * SPAN : (u + 1) * SPAN], tab_s[:].indirect(entries))
+        for u in range(HALVES):
+            gather_tab(1, u)
         load_w1(1, 1, 0)
         load_w1(2, 1, W_BYTES)
         cast_w1(1, 0, 0)

@@ -67,6 +67,7 @@ def tile_list_titanium_shock_pairs_kernel(
             x_f0[:, : PACK * PAIRS].rearrange("p (t m) -> p t m", t=PACK),
             x_f1[:].rearrange("p (t m) -> p t m", t=PACK),
         ]
+        v_s = {}
         tab_w, gain_row, v_c, w_raw, w_bf, w_c, w_s = {}, {}, {}, {}, {}, {}, {}
         h_sum, h, x_bf, x_c, x_s, total = {}, {}, {}, {}, {}, {}
         halves = [(0, MID), (MID, PAIRS)]
@@ -135,6 +136,11 @@ def tile_list_titanium_shock_pairs_kernel(
             entries = offs_sb[:, u * SPAN // PER_COLUMN : (u + 1) * SPAN // PER_COLUMN]
             nc.vector.tensor_copy(v_c[a, u][:], tab_w[a][:].bitcast(U32).indirect(entries))
 
+        def gather_scales(u, offset):
+            v_s[u] = areas.tile([P, SPAN], U8, name="v_s%d" % u, offset=offset, align_bytes=64)
+            entries = offs_sb[:, u * SPAN // PER_COLUMN : (u + 1) * SPAN // PER_COLUMN]
+            nc.vector.tensor_copy(v_s[u][:], tab_s[:].indirect(entries))
+
         def first_product(a, b, t, u):
             if a == 0:
                 h_sum[b, t, u] = psum.tile([P, SPAN], F32, name="bank")
@@ -143,7 +149,7 @@ def tile_list_titanium_shock_pairs_kernel(
                 lhsT=w_c[a, b, t].bitcast(FP8X4),
                 lhsT_scale=w_s[a, b, t],
                 rhs=v_c[a, u][:].bitcast(FP8X4),
-                rhs_scale=v_s[PACK * (a + 1) :, u * SPAN : (u + 1) * SPAN],
+                rhs_scale=v_s[u][PACK * (a + 1) :, :],
                 start=(a == 0),
                 stop=(a == K_PASSES - 1),
             )
@@ -217,18 +223,16 @@ def tile_list_titanium_shock_pairs_kernel(
             out=w4_s[:].rearrange("p a (c t m) -> p (a c) t m", t=PACK, m=P),
             in_=w4_raw_s[:].rearrange("p a (c m t) -> p (a c) t m", t=PACK, m=P),
         )
-        v_s = areas.tile([P, S], U8, name="v_s", offset=TAB_BYTES, align_bytes=64)
-        for u in range(HALVES):
-            entries = offs_sb[:, u * SPAN // PER_COLUMN : (u + 1) * SPAN // PER_COLUMN]
-            nc.vector.tensor_copy(v_s[:, u * SPAN : (u + 1) * SPAN], tab_s[:].indirect(entries))
+        gather_scales(0, TAB_BYTES)
+        cast_w1(1, 0, 0)
+        load_w1(1, 1, W_AREA + W_BYTES)
+        quantize_w1(1, 0, ALL_TILES)
         for u in range(HALVES):
             gather_tab(1, u)
-        load_w1(1, 1, 0)
-        load_w1(2, 1, W_BYTES)
-        cast_w1(1, 0, 0)
-        quantize_w1(1, 0, ALL_TILES)
-        for a in range(K_PASSES - 1):
-            for u in range(HALVES):
+        gather_scales(1, W_BYTES)
+        load_w1(2, 1, 0)
+        for u in range(HALVES):
+            for a in range(K_PASSES - 1):
                 for t in range(PACK):
                     first_product(a, 0, t, u)
         for u in range(HALVES):

from contextlib import ExitStack

import concourse.mybir as mybir

K, T, S, PAIRS, H = 1536, 4096, 1024, 512, 1024
FLOPS = 2 * K * H * S + 2 * H * H * PAIRS

F32 = mybir.dt.float32
BF16 = mybir.dt.bfloat16
I32 = mybir.dt.int32
U32 = mybir.dt.uint32
U16 = mybir.dt.uint16
U8 = mybir.dt.uint8
FP8X4 = mybir.dt.float8_e4m3fn_x4
FP4X4 = mybir.dt.float4_e2m1fn_x4
ACT = mybir.ActivationFunctionType
ALU = mybir.AluOpType

P = 128
PACK = 4
SPAN = P * PACK
K_PASSES = K // SPAN
BLOCKS = H // SPAN
HALVES = S // SPAN
QUADRANT = 32
QUADRANTS = P // QUADRANT
PER_COLUMN = 16
MID = PAIRS // 2
RUN = 4
ALL_TILES = [(0, PACK)]
TILE_PAIRS = [(0, 2), (2, PACK)]
FIRST_TILES_FIRST = [(0, 1), (1, 2), (2, PACK)]
EARLY_TILES = 2
SQRT_LAG = 2

PAIR_CAST_ON_VECTOR = (56, 40)
LAST_CAST_ON_VECTOR = (84, 40)

TAB_BYTES = 4 * T
W_BYTES = 4 * PACK * SPAN
W_AREA = K_PASSES * TAB_BYTES


def tile_list_titanium_shock_pairs_kernel(
    tc, tab_words, tab_scales, offs, pos1, pos2, w1, w4_words, w4_scales, gain, out
):
    nc = tc.nc
    with ExitStack() as ctx:
        keep = ctx.enter_context(tc.tile_pool(name="keep", bufs=1))
        areas = ctx.enter_context(tc.tile_pool(name="areas", bufs=1))
        stage = ctx.enter_context(tc.tile_pool(name="stage", bufs=2))
        psum = ctx.enter_context(tc.psum_pool(name="psum", bufs=8))

        offs_sb = keep.tile([P, S // PER_COLUMN], U16, name="offs_sb")
        pos1_sb = keep.tile([P, PAIRS // PER_COLUMN], U16, name="pos1_sb")
        pos2_sb = keep.tile([P, PAIRS // PER_COLUMN], U16, name="pos2_sb")
        tab_s = keep.tile([P, T], U8, name="tab_s")
        w4_raw_s = keep.tile([P, BLOCKS, H], U8, name="w4_raw_s")
        w4_c = keep.tile([P, BLOCKS, 2 * H], U8, name="w4_c", align_bytes=64)
        w4_s = keep.tile([P, BLOCKS, H], U8, name="w4_s", align_bytes=64)
        gain_sb = keep.tile([P, BLOCKS, PACK], F32, name="gain_sb")
        eps = keep.tile([P, 1], F32, name="eps")
        x_f0 = keep.tile([P, (PACK - 1) * PAIRS + PACK * SPAN], F32, name="x_f0", align_bytes=64)
        late_bf = x_f0[:, (PACK - 1) * PAIRS :].bitcast(BF16)
        x_f1 = keep.tile([P, PACK * PAIRS], F32, name="x_f1", align_bytes=64)
        x_f = [
            x_f0[:, : PACK * PAIRS].rearrange("p (t m) -> p t m", t=PACK),
            x_f1[:].rearrange("p (t m) -> p t m", t=PACK),
        ]
        v_s = {}
        tab_w, gain_row, v_c, w_raw, w_bf, w_c, w_s = {}, {}, {}, {}, {}, {}, {}
        h_sum, h, x_bf, x_c, x_s, total = {}, {}, {}, {}, {}, {}
        halves = [(0, MID), (MID, PAIRS)]

        def load_w1(a, b, offset, queue=nc.sync):
            w_raw[a, b] = areas.tile([P, PACK, SPAN], F32, name="w_raw%d%d" % (a, b), offset=offset)
            rows = w1[a * SPAN : (a + 1) * SPAN, b * SPAN : (b + 1) * SPAN]
            queue.dma_start(out=w_raw[a, b][:], in_=rows.rearrange("(p j) c -> p j c", j=PACK))

        def load_tab(a):
            tab_w[a] = areas.tile([P, T], I32, name="tab_w%d" % a, offset=(1, 0, 2)[a] * TAB_BYTES)
            nc.sync.dma_start(out=tab_w[a][:], in_=tab_words[a].rearrange("p t i -> p (t i)").bitcast(I32))

        def cast_views(a, b):
            if a > 0 and b == 1:
                dst = late_bf.rearrange("p (t a m j) -> p a m j t", t=PACK, a=2, j=PACK)[:, a - 1]
            else:
                if b == 1:
                    w_bf[a, b] = x_f0[:, PAIRS : 3 * PAIRS].bitcast(BF16)
                else:
                    w_bf[a, b] = stage.tile([P, PACK * SPAN], BF16, name="w_bf", align_bytes=64)[:]
                dst = w_bf[a, b].rearrange("p (t m j) -> p m j t", t=PACK, j=PACK)
            src = w_raw[a, b][:].rearrange("p j (m t) -> p m j t", t=PACK)
            return dst, src

        def cast_w1(a, b, on_vector):
            dst, src = cast_views(a, b)
            if on_vector > 0:
                nc.vector.tensor_copy(out=dst[:, :on_vector], in_=src[:, :on_vector])
            if on_vector < P:
                nc.scalar.copy(out=dst[:, on_vector:], in_=src[:, on_vector:])

        def cast_w1_by_pairs(a, b, shares):
            dst, src = cast_views(a, b)
            for (t0, t1), on_vector in zip(TILE_PAIRS, shares):
                nc.vector.tensor_copy(out=dst[:, :on_vector, :, t0:t1], in_=src[:, :on_vector, :, t0:t1])
                nc.scalar.copy(out=dst[:, on_vector:, :, t0:t1], in_=src[:, on_vector:, :, t0:t1])

        def quantize(codes, scales, values):
            nc.vector.quantize_mx(out=codes.bitcast(FP8X4), scales=scales, in_=values)

        def quantize_w1(a, b, tile_runs):
            codes = keep.tile([P, SPAN], U32, name="w_c%d%d" % (a, b), align_bytes=64)
            scales = keep.tile([P, SPAN], U8, name="w_s%d%d" % (a, b), align_bytes=64)
            for t0, t1 in tile_runs:
                cols = slice(t0 * P, t1 * P)
                quantize(codes[:, cols], scales[:, cols], w_bf[a, b][:, t0 * SPAN : t1 * SPAN])
            for t in range(PACK):
                w_c[a, b, t] = codes[:, t * P : (t + 1) * P]
                w_s[a, b, t] = scales[:, t * P : (t + 1) * P]

        def quantize_late():
            codes = keep.tile([P, 2 * SPAN], U32, name="late_c", tag="x_bf0", align_bytes=64)
            scales = keep.tile([P, 2 * SPAN], U8, name="late_s", align_bytes=64)
            for t0, t1 in FIRST_TILES_FIRST:
                cols = slice(2 * t0 * P, 2 * t1 * P)
                quantize(codes[:, cols], scales[:, cols], late_bf[:, 2 * t0 * SPAN : 2 * t1 * SPAN])
            for t in range(PACK):
                for a in (1, 2):
                    cols = slice((2 * t + a - 1) * P, (2 * t + a) * P)
                    w_c[a, 1, t] = codes[:, cols]
                    w_s[a, 1, t] = scales[:, cols]

        def gather_tab(a, u):
            v_c[a, u] = keep.tile([P, SPAN], U32, name="v_c%d%d" % (a, u), align_bytes=64)
            entries = offs_sb[:, u * SPAN // PER_COLUMN : (u + 1) * SPAN // PER_COLUMN]
            nc.vector.tensor_copy(v_c[a, u][:], tab_w[a][:].bitcast(U32).indirect(entries))

        def gather_scales(u, offset):
            v_s[u] = areas.tile([P, SPAN], U8, name="v_s%d" % u, offset=offset, align_bytes=64)
            entries = offs_sb[:, u * SPAN // PER_COLUMN : (u + 1) * SPAN // PER_COLUMN]
            nc.vector.tensor_copy(v_s[u][:], tab_s[:].indirect(entries))

        def first_product(a, b, t, u):
            if a == 0:
                h_sum[b, t, u] = psum.tile([P, SPAN], F32, name="bank")
            nc.tensor.matmul_mx(
                out=h_sum[b, t, u][:],
                lhsT=w_c[a, b, t].bitcast(FP8X4),
                lhsT_scale=w_s[a, b, t],
                rhs=v_c[a, u][:].bitcast(FP8X4),
                rhs_scale=v_s[u][PACK * (a + 1) :, :],
                start=(a == 0),
                stop=(a == K_PASSES - 1),
            )

        def square_h(b, t):
            h[b, t] = keep.tile([P, S], F32, name="h%d%d" % (b, t))
            for u in range(HALVES):
                nc.scalar.activation(out=h[b, t][:, u * SPAN : (u + 1) * SPAN], in_=h_sum[b, t, u][:], func=ACT.Square)

        def pick_x(b, t, m0=0, m1=PAIRS):
            entries = pos1_sb[:, m0 // PER_COLUMN : m1 // PER_COLUMN]
            nc.vector.tensor_tensor(
                x_f[b][:, t, m0:m1], h[b, t][:].indirect(entries), gain_row[b, t][:, m0:m1], ALU.mult
            )

        def round_x(b, m0, m1):
            if b == 0:
                dst = x_bf[b, m0].rearrange("p (m t) -> p m t", t=PACK)
                nc.scalar.copy(out=dst, in_=x_f[b][:, :, m0:m1].rearrange("p t m -> p m t"))
            else:
                dst = x_bf[b, m0].rearrange("p (c i t) -> p c t i", i=RUN, t=PACK)
                nc.vector.tensor_copy(out=dst, in_=x_f[b][:, :, m0:m1].rearrange("p t (c i) -> p c t i", i=RUN))

        def quantize_x(b, m0, m1):
            if m0 == 0:
                x_c[b] = keep.tile([P, PAIRS], U32, name="x_c%d" % b, align_bytes=64)
                x_s[b] = keep.tile([P, PAIRS], U8, name="x_s%d" % b, align_bytes=64)
            quantize(x_c[b][:, m0:m1], x_s[b][:, m0:m1], x_bf[b, m0])

        load_w1(0, 0, W_AREA, nc.scalar)
        load_w1(1, 0, W_AREA + W_BYTES, nc.scalar)
        nc.vector.memset(tab_s[:].bitcast(I32), 0)
        nc.gpsimd.memset(w4_raw_s[:].bitcast(I32), 0)
        nc.vector.memset(eps[:], 0.25)
        warm = keep.tile([P, 1], F32, name="warm")
        nc.scalar.activation(out=warm[:], in_=eps[:], func=ACT.Sqrt)

        load_tab(0)
        nc.sync.dma_start(offs_sb[:], offs)
        for q in range(QUADRANTS):
            nc.gpsimd.dma_start(
                out=tab_s[QUADRANT * q + PACK : QUADRANT * q + PACK * (K_PASSES + 1), :].bitcast(I32),
                in_=tab_scales[:, PACK * q : PACK * (q + 1), :].bitcast(I32),
            )
            nc.sync.dma_start(
                out=w4_raw_s[QUADRANT * q : QUADRANT * q + PACK, :, :].bitcast(I32),
                in_=w4_scales[:, PACK * q : PACK * (q + 1), :].rearrange("a r n -> r a n").bitcast(I32),
            )
        nc.sync.dma_start(out=gain_sb[:], in_=gain.rearrange("(b p t) -> p b t", p=P, t=PACK))
        load_tab(1)
        load_tab(2)
        load_w1(2, 0, W_AREA + 2 * W_BYTES)
        nc.sync.dma_start(pos1_sb[:], pos1)
        nc.sync.dma_start(pos2_sb[:], pos2)
        w4_raw = keep.tile([P, BLOCKS, 2 * H], U8, name="w4_raw")
        nc.sync.dma_start(out=w4_raw[:].bitcast(I32), in_=w4_words.rearrange("a p n -> p a n").bitcast(I32))

        cast_w1(0, 0, 0)
        load_w1(0, 1, W_AREA)
        for b in range(BLOCKS):
            for t in range(PACK):
                if (b, t) == (0, 0):
                    gain_row[b, t] = x_f0[:, PAIRS : 2 * PAIRS]
                else:
                    gain_row[b, t] = keep.tile([P, PAIRS], F32, name="gain_row%d%d" % (b, t))[:]
                nc.scalar.copy(out=gain_row[b, t], in_=gain_sb[:, b, t : t + 1].to_broadcast([P, PAIRS]))
        quantize_w1(0, 0, ALL_TILES)
        for u in range(HALVES):
            gather_tab(0, u)
        nc.vector.tensor_copy(
            out=w4_s[:].rearrange("p a (c t m) -> p (a c) t m", t=PACK, m=P),
            in_=w4_raw_s[:].rearrange("p a (c m t) -> p (a c) t m", t=PACK, m=P),
        )
        gather_scales(0, TAB_BYTES)
        cast_w1(1, 0, 0)
        load_w1(1, 1, W_AREA + W_BYTES)
        quantize_w1(1, 0, ALL_TILES)
        for u in range(HALVES):
            gather_tab(1, u)
        gather_scales(1, W_BYTES)
        load_w1(2, 1, 0)
        for u in range(HALVES):
            for a in range(K_PASSES - 1):
                for t in range(PACK):
                    first_product(a, 0, t, u)
        for u in range(HALVES):
            gather_tab(2, u)
        cast_w1_by_pairs(2, 0, PAIR_CAST_ON_VECTOR)
        quantize_w1(2, 0, TILE_PAIRS)
        for t in range(PACK):
            for u in range(HALVES):
                first_product(2, 0, t, u)
        nc.vector.tensor_copy(
            out=w4_c[:].bitcast(U16).rearrange("p a (c t m) -> p (a c) t m", t=PACK, m=P),
            in_=w4_raw[:].bitcast(U16).rearrange("p a (c m t) -> p (a c) t m", t=PACK, m=P),
        )
        for t in range(PACK):
            square_h(0, t)

        pick_x(0, 0)
        dst, src = cast_views(0, 1)
        for t0, t1 in TILE_PAIRS:
            nc.vector.tensor_copy(out=dst[:, :, :, t0:t1], in_=src[:, :, :, t0:t1])
        quantize_w1(0, 1, TILE_PAIRS)
        cast_w1(1, 1, 0)
        pick_x(0, 1)
        pick_x(0, 2)
        cast_w1_by_pairs(2, 1, LAST_CAST_ON_VECTOR)
        quantize_late()
        pick_x(0, 3)
        for t in range(PACK):
            for u in range(HALVES):
                first_product(0, 1, t, u)
        for t in range(PACK):
            for u in range(HALVES):
                for a in range(1, K_PASSES):
                    first_product(a, 1, t, u)
        for t in range(PACK):
            square_h(1, t)
            if t < PACK - 1:
                pick_x(1, t)
        x_bf0 = keep.tile([P, PAIRS * PACK], BF16, name="x_bf0", tag="x_bf0", align_bytes=64)
        x_bf1 = keep.tile([P, MID * PACK], BF16, name="x_bf1", align_bytes=64)
        x_bf[0, 0], x_bf[0, MID] = x_bf0[:, : MID * PACK], x_bf0[:, MID * PACK :]
        x_bf[1, 0], x_bf[1, MID] = x_bf1[:], x_bf[0, 0]
        for m0, m1 in halves:
            pick_x(1, PACK - 1, m0, m1)
        for m0, m1 in halves:
            for b in range(BLOCKS):
                round_x(b, m0, m1)
            for b in range(BLOCKS):
                quantize_x(b, m0, m1)

        out_rows = out.rearrange("(b p t) m -> b t p m", p=P, t=PACK)
        row_tiles = [(b, t) for b in range(BLOCKS) for t in range(PACK)]

        def second_product(b, t, m0, m1):
            y = psum.tile([P, m1 - m0], F32, name="bank")
            col = b * SPAN + t * P
            width = PAIRS if m1 - m0 == PAIRS else P
            for m in range(m0, m1, width):
                for a in range(BLOCKS):
                    nc.tensor.matmul_mx(
                        out=y[:, m - m0 : m - m0 + width],
                        lhsT=w4_c[:, a, 2 * col : 2 * (col + P)].bitcast(FP4X4),
                        lhsT_scale=w4_s[:, a, col : col + P],
                        rhs=x_c[a][:, m : m + width].bitcast(FP8X4),
                        rhs_scale=x_s[a][:, m : m + width],
                        start=(a == 0),
                        stop=(a == BLOCKS - 1),
                    )
            y_sq = stage.tile([P, m1 - m0], F32, name="y_sq", bufs=SQRT_LAG + 2)
            nc.scalar.activation(out=y_sq[:], in_=y[:], func=ACT.Square)
            if m0 == 0:
                offset = 2 * TAB_BYTES + 4 * PAIRS * (PACK * b + t)
                total[b, t] = areas.tile([P, PAIRS], F32, name="total%d%d" % (b, t), offset=offset)
            for n0, n1 in pieces(b, t, m0, m1):
                nc.vector.tensor_tensor(
                    total[b, t][:, n0:n1],
                    h[b, t][:].indirect(pos2_sb[:, n0 // PER_COLUMN : n1 // PER_COLUMN]),
                    y_sq[:, n0 - m0 : n1 - m0],
                    ALU.add,
                )

        def pieces(b, t, m0, m1):
            return halves if (b, t) == row_tiles[-1] else [(m0, m1)]

        def finish(b, t):
            for m0, m1 in pieces(b, t, 0, PAIRS):
                part = total[b, t][:, m0:m1]
                nc.scalar.activation(out=part, in_=part, func=ACT.Sqrt, bias=eps[:])
                queue = nc.scalar if ((b, t), m1) == (row_tiles[-1], PAIRS) else nc.sync
                queue.dma_start(out=out_rows[b, t][:, m0:m1], in_=part)

        for m0, m1 in halves:
            for b, t in row_tiles[:EARLY_TILES]:
                second_product(b, t, m0, m1)
        for i in range(EARLY_TILES, len(row_tiles) + SQRT_LAG):
            if i < len(row_tiles):
                second_product(*row_tiles[i], 0, PAIRS)
            finish(*row_tiles[i - SQRT_LAG])
